import numpy as np, ml_dtypes
CORES = [9,25,41,57]
N = 4
import mx_ref
BF = ml_dtypes.bfloat16
def entries(a):
    return np.ascontiguousarray(a.T).reshape(-1)
def table(e):
    return np.ascontiguousarray(np.reshape(e, (-1, 16)).T).astype(np.int32)
def pick(q, e):
    c = np.concatenate([q[0].reshape(128, -1, 4), np.zeros((128, 1, 4), np.uint8)], axis=1); s = np.concatenate([q[1], np.ones((16, 1), np.uint8)], axis=1)
    return (np.ascontiguousarray(c[:, e].reshape(128, -1)), np.ascontiguousarray(s[:, e]))
def join(*qs):
    return (np.concatenate([q[0] for q in qs], axis=1), np.concatenate([q[1] for q in qs], axis=1))
def put(q, e, v):
    c, s = q[0].reshape(128, -1, 4).copy(), q[1].copy(); c[:, e] = v[0].reshape(128, -1, 4); s[:, e] = v[1]
    return (c.reshape(128, -1), s)
def pk(c, s):
    return (np.ascontiguousarray(c), mx_ref.live(s))
def emit(q):
    return q[0], q[1]
def packed(v, rng):
    q = [mx_ref.quantize(np.ascontiguousarray(v[r])) for r in range(N)]
    return np.stack([a for a, b in q]), np.stack([mx_ref.plane(b, rng) for a, b in q])
def cols(t, e):
    v = np.concatenate([t.reshape(128, -1, 4), np.zeros((128, 1, 4), BF)], axis=1)
    return np.ascontiguousarray(v[:, e]).reshape(128, -1)
def f(rng, *shape):
    return mx_ref.flush((rng.standard_normal(shape, dtype=np.float32) * np.exp2(rng.integers(-2, 3, shape[:-1] + (1,)))).astype(BF))
def wide(rng, *shape, cols=0):
    v = rng.standard_normal(shape, dtype=np.float32) * np.exp2(rng.integers(-12, 13, shape)).astype(np.float32)
    if cols: v *= np.repeat(np.exp2(rng.integers(-cols, cols + 1, shape[:-2] + (1, shape[-1] // 4))) * (rng.random(shape[:-2] + (1, shape[-1] // 4)) > 0.0625), 4, axis=-1).astype(np.float32)
    return mx_ref.flush(v.astype(BF))
T, C, CAPP, M = 512, 1024, 96, 256
def first(v):
    z = np.zeros((N, 128, 512), BF); z[:, :, :4] = v; return z
def lists(rng, full=False, one=False, odd=False):
    h = int(rng.integers(0, N)); a = rng.permutation(np.delete(np.arange(N), h))
    sn = np.full((N, N, CAPP), -1)
    for d in range(N):
        m, o = int(rng.integers(1, M + 1)), rng.permutation(N * CAPP)
        if odd: m = 2 * int(rng.integers(0, M // 2)) + 1
        if full:
            w = np.isin(o // CAPP, a[:M // CAPP] if d == h else a[:1]); o = np.concatenate([o[w], o[~w]])
            m = M if d == h else int(rng.integers(CAPP, M + 1))
        if one: o = o[o // CAPP != a[0]]
        if one and d == h: m, o = 1, o[o // CAPP != h]
        o = o[:m]
        sn[o // CAPP, d, o % CAPP] = rng.integers(0, T, m)
    return np.stack([table(sn[s]) for s in range(N)])
def setup_inputs(rng):
    kc, ks = packed(f(rng, N, 128, 4 * C), rng)
    return {"x": f(rng, N, 128, 4 * T), "u": first(f(rng, N, 128, 4)), "w": f(rng, N, 128, 512), "kc": kc, "ks": ks, "sn": lists(rng)}
def setup_inputs_full(rng):
    return {**setup_inputs(rng), "sn": lists(rng, full=True)}
def setup_inputs_high(rng):
    d = setup_inputs(rng); g = np.where(rng.permutation(N) < N // 2, 1, -1).astype(np.float32)[:, None, None]
    p = rng.permutation(N)
    g = g * np.where(p < N // 2, 2.0 ** 24, 2.0 ** -24).astype(np.float32)[:, None, None]
    k = np.where(p == N - 1, 2.0 ** -24, 2.0 ** 24).astype(np.float32)[:, None, None]
    d["u"] = first(((np.abs(f(rng, N, 128, 4).astype(np.float32)) + 1) * k).astype(BF))
    d["kc"], d["ks"] = packed((g * (1 + np.abs(f(rng, N, 128, 4 * C).astype(np.float32)))).astype(BF), rng); return d
def setup_inputs_one(rng):
    return {**setup_inputs(rng), "sn": lists(rng, one=True)}
def setup_inputs_spread(rng):
    d = setup_inputs(rng); d["x"] = wide(rng, N, 128, 4 * T, cols=8)
    d["kc"], d["ks"] = packed(wide(rng, N, 128, 4 * C, cols=8), rng); return d
def setup_inputs_ties(rng):
    d = setup_inputs(rng); v = f(rng, N, 128, C // 8 * 4)
    d["kc"], d["ks"] = packed(np.stack([cols(v[r], rng.permutation(np.arange(C) // 8)) for r in range(N)]), rng)
    d["u"][int(rng.integers(0, N))] = 0
    d["sn"] = lists(rng, odd=True); return d
def scores(u, kc, ks):
    return mx_ref.matmul(mx_ref.quantize(np.ascontiguousarray(u)), pk(kc, ks))[0] + np.float32(0)
def check_inputs(d):
    b = []
    for r in range(N):
        if (d["u"][r][:, 4:].astype(np.float32) != 0).any(): b.append("u")
        e = entries(d["sn"][r])
        m = sum(int((entries(d["sn"][s])[r * CAPP:r * CAPP + CAPP] >= 0).sum()) for s in range(N))
        if e.min() < -1 or e.max() >= T or m < 1 or m > M: b.append("sn")
        try: good = bool(np.isfinite(scores(d["u"][r], d["kc"][r], d["ks"][r])).all())
        except Exception: good = False
        if not good: b.append("kc")
    return b
def reference(x, u, w, kc, ks, sn):
    oc, osc, ev = np.zeros((N, 128, 4 * C), np.uint8), np.zeros((N, 16, C), np.uint8), np.zeros((N, 2, M), np.float32)
    y = np.zeros((N, 128, C), np.float32)
    new = join(*[mx_ref.quantize(np.ascontiguousarray(x[s])) for s in range(N)])
    for d in range(N):
        e = []
        for s in range(N):
            v = entries(sn[s])[d * CAPP:d * CAPP + CAPP]; e.append(s * T + v[v >= 0])
        e = np.concatenate(e); m = e.size
        z = scores(u[d], kc[d], ks[d])
        out = np.argsort(z, kind="stable")[:m]
        after = put(pk(kc[d], ks[d]), out, pick(new, e))
        oc[d], osc[d] = emit(after)
        ev[d, 0] = -1; ev[d, 0, :m] = out; ev[d, 1, :m] = z[out]
        y[d] = mx_ref.matmul(mx_ref.quantize(np.ascontiguousarray(w[d])), after)
    return {"oc": oc, "osc": osc, "ev": ev, "y": y}

@@ -1,0 +1,302 @@
+from concourse.bass import DstId, RemoteDMATransfer
+from concourse.mybir import dt, AluOpType as ALU, ActivationFunctionType as ACT
+
+NR, NT, NC, CAP, MX = 4, 512, 1024, 96, 256
+NW = NC + NR * CAP
+LC = CAP // 16
+BLK = [3, 7, 2, 6, 1, 5, 0, 4]
+NS = 3
+VP, SP = [[4, 6], [3, 5, 7]], [[0, 2], [1]]
+WD = NC + 128
+TINY = 2.0 ** -120
+NP, PW = 4, 256
+UC = 14
+
+SCRATCH = {"psv": ("psum", [128, 1024], "float32"), "pss": ("psum", [128, 1024], "float32"), "py": ("psum", [128, 2048], "float32")}
+_SPEC = {
+    "float8_e4m3fn_x4": "uq 144 urq 128 xq 512 wq 128 sndq 384 winq 1408 aftq 1024",
+    "uint8": "us 144 urs 128 xs 512 wsc 128 snds 384 wins 1408 afts 1024",
+    "int32": "sn8 24 ll 24 pi 8 pa 2 vo0 8 kk0 16 kk1 16",
+    "uint16": "su 24 lu 24 ul 8 rkd 16 rkn 8 off 64 vo 8 pm 4",
+    "bfloat16": "u0 16 ua 576 xt 2048 wt 512 eq 1024 eqm 384 w01 528 fl 384 incl 384 csg 768 cm3 1152 cm4 1152 cm5 1152 cm6 1152 cm7 1152 sg0 1024 sg1 1024 sg2 1024",
+    "float16": "co 192 scn 4608",
+    "float32": "df0 1024 df1 1024 df2 1024 scol 8 acc1 4 acc2 4 base 4 csum 2 ksl 2 kfl 2 a2 64 b2 64 "
+               "pos 264 pt 256 it 64 tt 64 ysb 1024 pf 2 kcol 2 kcoh 2 js 256 vj 128 vs 128 pm0 4 kk 16 "
+               "sr 1024 ej 1024 es 1024 er 128 e0 64 e1 32 e2 16 e3 16 e4 16 em 16 eg 16",
+}
+for _d in _SPEC:
+    _w = _SPEC[_d].split()
+    for _i in range(0, len(_w), 2):
+        SCRATCH[_w[_i]] = ("sbuf", [128, int(_w[_i + 1])], _d)
+SEMAPHORES = "qv qs qt qg lsn lu0 lk0 lk1 lk2 lx lw lown own hop evx sto larr carr sent".split()
+
+
+def rank_program(g, core, T, topo):
+    me = T.rank_of(core)
+    if me is None:
+        return
+    seen, total = {}, {}
+    v, queues = g.vector, {"v": g.vector, "s": g.scalar, "t": g.tensor, "g": g, "y": g.sync}
+    u8, u32, FL = dt.uint8, dt.uint32, {"allow_small_or_imprecise_dtypes": True}
+
+    def wait(q, deps):
+        for name, val in deps:
+            if seen.get((q, name), 0) < val:
+                queues[q].wait_ge(T.sem[name], val)
+                seen[(q, name)] = val
+
+    def tick(name, n):
+        total[name] = total.get(name, 0) + n
+        return (name, total[name])
+
+    def V(deps, f, *a):
+        wait("v", deps); f(*a).then_inc(T.sem.qv, 1); return tick("qv", 1)
+
+    def S(deps, out, in_, func, **k):
+        wait("s", deps); g.scalar.activation(out, in_, func, **k).then_inc(T.sem.qs, 1); return tick("qs", 1)
+
+    def P(deps, *a):
+        wait("t", deps); g.tensor.matmul_mx(*a).then_inc(T.sem.qt, 1); return tick("qt", 1)
+
+    def G(deps, f, *a, **k):
+        wait("g", list(deps) + [("qg", total.get("qg", 0))]); f(*a, **k).then_inc(T.sem.qg, 1); return tick("qg", 1)
+
+    def D(q, deps, sem, out, in_):
+        wait(q, deps); queues[q].dma_start(out, in_).then_inc(T.sem[sem], 16); return tick(sem, 16)
+
+    kl = []
+    for i, (a, b) in enumerate(((0, 256), (256, 512), (512, 1024))):
+        D("y", [], "lk%d" % i, T.winq[:, a:b].bitcast(u8), T.kc[:, 4 * a:4 * b])
+        kl.append(D("y", [], "lk%d" % i, T.wins[:, a:b], T.ks[:, a:b]))
+    u0 = D("s", [], "lu0", T.u0[:], T.u[:, 0:16])
+    for q in range(8):
+        sn = D("s" if q < 6 else "y", [], "lsn", T.sn8[16 * q:16 * q + 16, :], T.sn[:])
+    xl = D("y", [], "lx", T.xt[:], T.x[:])
+    wl = D("y", [], "lw", T.wt[:], T.w[:])
+
+    G([], g.iota, T.pi[:, 0:4], [[0, 4]], 0, 1)
+    c_p = G([], g.iota, T.pi[:, 4:8], [[0, 4]], 0, 4)
+    c_pm = G([], g.iota, T.pm0[:], [[32, 2], [-2, 2]], 3, 0, **FL)
+    c_kk = G([], g.iota, T.kk0[0:32, :], [[1, 16]], 0, 16)
+    for a in range(4):
+        c_k = G([], g.iota, T.kcol[32 * a:32 * a + 32, :], [[32, 2]], 64 * a, 1, **FL)
+    c_vo = G([], g.iota, T.vo0[:], [[-128, 4], [512, 2]], 384, 1)
+    for b in range(4):
+        c_js = G([], g.iota, T.js[:, 64 * b:64 * b + 64], [[512, 2], [0, 2], [1, 16]], 384 - 128 * b, 1, **FL)
+    c_vj = G([], g.iota, T.vj[:], [[-128, 4], [512, 2], [1, 16]], 384, 1, **FL)
+
+    others = [d for d in range(NR) if d != me]
+    emask = {d: sum(1 << e for e in topo.engines(core, T.cores[d])[2 * i:2 * i + 2]) for i, d in enumerate(others)}
+
+    def send(deps, sem, src, dst):
+        wait("g", deps)
+        tr = []
+        for d in others:
+            rid, pid = topo.addr(T.cores[d])[0:2]
+            tr.append(RemoteDMATransfer(dst_ids=[DstId(rid=rid, pnc=pid)], dma_engine_mask=emask[d], remote_sem=T.sem[sem],
+                                        src=src(d), dst=dst(d)))
+        g.remote_dma_fused(tr, local_sem=T.sem.sent)
+        tick("sent", 2 * len(others))
+
+    send([sn], "larr", lambda d: T.sn8[:, LC * d:LC * d + LC], lambda d: T.ll[:, LC * me:LC * me + LC])
+    larr = tick("larr", 2 * len(others))
+    lown = D("y", [sn], "lown", T.ll[:, LC * me:LC * me + LC], T.sn8[:, LC * me:LC * me + LC])
+
+    z_u = V([], v.memset, T.ua[:], 0.0)
+    z_l = V([], v.memset, T.ul[:], UC)
+    t = V([u0, z_u], v.tensor_copy, T.ua[:, 4 * UC:4 * UC + 4], T.u0[:, 0:4])
+    uq = V([t], v.quantize_mx, T.uq[:], T.us[:], T.ua[:])
+    ur = V([uq, z_l], v.tensor_copy, T.urq[:].bitcast(u32), T.uq[:].bitcast(u32).indirect(T.ul[:]))
+    S([z_u], T.w01[:, 1:513], T.ua[:, 64:576], ACT.Identity, bias=1.0, scale=0.0)
+    us = S([uq, z_l], T.urs[:], T.us[:].indirect(T.ul[:]), ACT.Copy)
+    z2 = S([], T.w01[:, 0:1], T.ua[:, 64:65], ACT.Copy)
+    z3 = S([], T.a2[:], T.ua[:, 64:128], ACT.Copy)
+    z8 = S([], T.pos[:, MX:MX + 8], T.ua[:, 64:72], ACT.Copy)
+    V([c_p], v.tensor_scalar, T.pa[:, 0:1], T.pi[:, 4:5], 28, None, ALU.bitwise_and)
+    a2 = V([], v.tensor_scalar, T.pa[:, 1:2], T.pi[:, 0:1], 3, 1, ALU.logical_shift_right, ALU.bitwise_and)
+    f7 = V([], v.tensor_scalar, T.pf[:, 1:2], T.pi[:, 0:1], 16, None, ALU.is_lt)
+    f6 = V([a2], v.tensor_tensor, T.pf[:, 0:1], T.pa[:, 0:1], T.pa[:, 1:2], ALU.subtract)
+    kk1 = V([c_kk], v.tensor_scalar, T.kk1[0:32, :], T.kk0[0:32, :], MX - 1, None, ALU.bitwise_and)
+    pm = V([f6, c_pm], v.tensor_scalar, T.pm[:], T.pm0[:], T.pf[:, 0:1], None, ALU.add)
+    kk = V([kk1], v.tensor_copy, T.kk[0:32, :], T.kk1[0:32, :])
+    kc = V([c_k], v.tensor_scalar, T.kcoh[:], T.kcol[:], 0.5, None, ALU.add)
+
+    def rows(ps, h):
+        a, b = 512 * h, 512 * h + 512
+        return P([ur, us, kl[h + 1]], ps[:, a:b], T.urq[:], T.urs[:], T.winq[:, a:b], T.wins[:, a:b], True, True)
+
+    sc = {}
+
+    def cols(bank, places, dep):
+        for i in places:
+            b, o = 128 * BLK[i], UC - 2 * i
+            sc[i] = P([uq, dep], T.py[:, 512 * bank:512 * bank + 128], T.winq[:, b:b + 128], T.wins[:, b:b + 128],
+                      T.uq[:, o:o + 128], T.us[:, o:o + 128], i == places[0], i == places[-1])
+
+    rv, rs = [], []
+    cols(0, VP[0], kl[0])
+    rv.append(rows(T.psv, 0))
+    cols(1, SP[0], kl[1])
+    rs.append(rows(T.pss, 0))
+    cols(2, VP[1], kl[2])
+    rv.append(rows(T.psv, 1))
+    cols(3, SP[1], kl[2])
+    rs.append(rows(T.pss, 1))
+
+    def columns(h, on_v):
+        places, bank = (VP if on_v else SP)[h], 512 * (2 * h + (not on_v))
+        i, j = places[0], places[-1] + 1
+        o, p, d = T.scol[:, i:j:2], T.py[:, bank + 2 * i:bank + 2 * j:4], [sc[places[-1]]]
+        t = V(d, v.tensor_copy, o, p) if on_v else S(d, o, p, ACT.Copy)
+        for k in places:
+            sc[k] = t
+
+    def s_diff(i, a, b):
+        return S([rs[a // 512], rs[(b - 1) // 512], sc[i]], T["df%d" % i][:, a:b], T.pss[:, a:b], ACT.Identity, bias=T.scol[:, i:i + 1], scale=-1.0)
+
+    def s_sign(i, d):
+        b, df, sg = 128 * BLK[i], T["df%d" % i], T["sg%d" % i]
+        S([d], sg[:, 0:b], df[:, 0:b], ACT.Sign, bias=TINY, accum_out=T.acc1[:, i:i + 1])
+        return S([d], sg[:, b:NC], df[:, b:NC], ACT.Sign, bias=-TINY, accum_out=T.acc2[:, i:i + 1])
+
+    def v_cmp(i, a, b):
+        m, cm, t = min(max(128 * BLK[i], a), b), T["cm%d" % i], None
+        for lo, hi, op in ((a, m, ALU.is_le), (m, b, ALU.is_lt)):
+            if lo < hi:
+                t = V([rv[lo // 512], rv[(hi - 1) // 512], sc[i]], v.tensor_scalar, cm[:, lo:hi], T.psv[:, lo:hi], T.scol[:, i:i + 1], 2.0, op, ALU.mult)
+        return t
+
+    def v_sum(i, c):
+        cm, o = T["cm%d" % i], WD // 2 * i
+        return V([c, eqm[i]], v.tensor_tensor_scan, T.scn[:, o:o + WD // 2], cm[:, 0:WD // 2], cm[:, WD // 2:WD], 0.0, ALU.add, ALU.add)
+
+    def v_eq(h, places):
+        for i in places:
+            b = 128 * BLK[i]
+            eqt[i] = V([sc[i], rv[h]], v.tensor_scalar, T.eq[:, 128 * i:128 * i + 128], T.psv[:, b:b + 128], T.scol[:, i:i + 1], 2.0, ALU.is_equal, ALU.mult)
+
+    def g_eq(i):
+        eqm[i] = G([eqt[i]], g.affine_select, T["cm%d" % i][:, NC:WD], T.eq[:, 128 * i:128 * i + 128], [[-1, 128]], ALU.is_gt, 0.0, 0, 1)
+
+    eqt, eqm = {}, {}
+    columns(0, True)
+    columns(0, False)
+    s_diff(0, 0, 512)
+    v_eq(0, VP[0])
+    s_diff(2, 0, 512)
+    for i in VP[0]:
+        g_eq(i)
+    v_cmp(4, 0, 512)
+    v_cmp(6, 0, 512)
+    v_eq(0, SP[0])
+    su = V([sn], v.tensor_copy, T.su[:], T.sn8[:])
+    columns(1, True)
+    columns(1, False)
+    v_eq(1, VP[1])
+    for i in VP[1]:
+        g_eq(i)
+    d0 = s_diff(0, 512, 1024)
+    s_sign(0, d0)
+    c4 = v_cmp(4, 512, 1024)
+    v_eq(1, SP[1])
+    eqs = G([eqt[1]], g.affine_select, T.eqm[:], T.eq[:, 0:128 * NS], [[0, NS], [-1, 128]], ALU.is_gt, 0.0, 0, 1)
+    xq = V([xl], v.quantize_mx, T.xq[:], T.xs[:], T.xt[:])
+    c6 = v_cmp(6, 512, 1024)
+    pq = V([xq, su], v.tensor_copy, T.sndq[:].bitcast(u32), T.xq[:].bitcast(u32).indirect(T.su[:]))
+    ps = S([xq, su], T.snds[:], T.xs[:].indirect(T.su[:]), ACT.Copy)
+    w0, own0 = NC + CAP * me, CAP * me
+    send([pq], "carr", lambda d: T.sndq[:, CAP * d:CAP * d + CAP].bitcast(u8), lambda d: T.winq[:, w0:w0 + CAP].bitcast(u8))
+    send([ps], "carr", lambda d: T.snds[:, CAP * d:CAP * d + CAP], lambda d: T.wins[:, w0:w0 + CAP])
+    carr = tick("carr", 4 * len(others))
+    D("y", [pq], "own", T.winq[:, w0:w0 + CAP].bitcast(u8), T.sndq[:, own0:own0 + CAP].bitcast(u8))
+    own = D("y", [ps], "own", T.wins[:, w0:w0 + CAP], T.snds[:, own0:own0 + CAP])
+    z6 = G([], g.iota, T.ej[:, 0:MX], [[0, MX]], 0, 0, **FL)
+    z7 = G([], g.iota, T.es[:, 0:MX], [[0, MX]], 0, 0, **FL)
+
+    v_sum(4, c4)
+    d2 = s_diff(2, 512, 1024)
+    lu = V([larr, lown], v.tensor_scalar, T.lu[:], T.ll[:], 1.0, None, ALU.add)
+    fl = S([lu, z2], T.fl[:], T.w01[:].indirect(T.lu[:]), ACT.Copy)
+    s_sign(2, d2)
+    c3 = v_cmp(3, 0, 1024)
+    v_sum(6, c6)
+    incl = V([fl], v.tensor_tensor_scan, T.incl[:], T.fl[:], T.fl[:], 0.0, ALU.add, ALU.max)
+    for h in range(2):
+        cs = S([incl, kc], T.csg[:, 384 * h:384 * h + 384], T.incl[:], ACT.Sign, bias=T.kcoh[:, h:h + 1], scale=-1.0, accum_out=T.csum[:, h:h + 1])
+    d1 = s_diff(1, 0, 1024)
+    c5 = v_cmp(5, 0, 1024)
+    sg = s_sign(1, d1)
+    v_sum(3, c3)
+    co, n64 = {}, float(NC)
+    for i in range(NS):
+        a = 128 * i
+        co[i] = V([eqs], v.tensor_tensor_scan, T.co[:, 64 * i:64 * i + 64], T.eqm[:, a:a + 64], T.eqm[:, a + 64:a + 128], n64, ALU.add, ALU.add)
+        if i == 0:
+            sl = V([cs], v.tensor_scalar, T.ksl[:], T.csum[:], 0.5, float(NC + NR * CAP // 2), ALU.mult, ALU.add)
+        if i == 1:
+            kf = V([sl], v.tensor_scalar, T.kfl[:], T.ksl[:], float(NW), None, ALU.is_lt)
+    km = V([kf, z3], v.tensor_tensor, T.a2[:, 0:64:32], T.ksl[:], T.kfl[:], ALU.mult)
+    v_sum(5, c5)
+    b2 = V([km], v.transpose, T.b2[:], T.a2[:])
+    for a in range(4):
+        pos = G([b2], g.partition_broadcast, T.pos[:, 64 * a:64 * a + 64], T.b2[32 * a:32 * a + 1, :], 128)
+    c7 = v_cmp(7, 0, 1024)
+    sm = v_sum(7, c7)
+    last, step = WD // 2 - 1, WD // 2
+    bs = V([sg, co[NS - 1]], v.tensor_tensor, T.base[:, 0:NS], T.co[:, 63:64 * NS:64], T.acc1[:, 0:NS], ALU.add)
+    cn = V([bs], v.tensor_tensor, T.scn[:, last:NS * step:step], T.base[:, 0:NS], T.acc2[:, 0:NS], ALU.add)
+    cnt = T.scn[:, last:8 * step:step]
+
+    V([cn, sm], v.tensor_scalar, T.rkd[:, 0:16:2], cnt, 0.5, float(MX), ALU.mult, ALU.min)
+    rd = V([], v.tensor_scalar, T.rkd[:, 1:16:2], cnt, 0.5, float(MX), ALU.mult, ALU.min)
+    rn = V([], v.tensor_scalar, T.rkn[:], cnt, 0.5, None, ALU.mult)
+    pt = V([rd, pos, z8, c_js], v.tensor_tensor, T.pt[:], T.pos[:].indirect(T.rkd[:]), T.js[:], ALU.max)
+    for a in range(4):
+        hop = D("y", [pt], "hop", T.it[32 * a:32 * a + 32, :], T.pt[0:128:16, :])
+
+    vo = V([c_vo], v.tensor_copy, T.vo[:], T.vo0[:])
+    sr = S([], T.sr[:], T.pss[:], ACT.Copy)
+    vs = S([sr, vo], T.vs[:], T.sr[:].indirect(T.vo[:]), ACT.Copy)
+    em = V([kk, incl], v.tensor_scalar, T.em[0:32, :], T.kk[0:32, :], T.incl[0:32, NR * CAP - 1:NR * CAP], None, ALU.is_lt)
+    ej = V([rn, z6, c_vj], v.tensor_copy, T.ej[:].indirect(T.rkn[:]), T.vj[:])
+    for q in range(8):
+        D("s", [ej], "evx", T.er[0:16, 16 * q:16 * q + 16], T.ej[16 * q:16 * q + 1, 0:MX])
+    wq = V([wl], v.quantize_mx, T.wq[:], T.wsc[:], T.wt[:])
+    eg = V([em, f7], v.tensor_scalar, T.eg[0:32, :], T.em[0:32, :], -1.0, T.pf[0:32, 1:2], ALU.add, ALU.mult)
+    es = V([vs, z7], v.tensor_copy, T.es[:].indirect(T.rkn[:]), T.vs[:])
+    for q in range(8):
+        evx = D("y", [es], "evx", T.er[16:32, 16 * q:16 * q + 16], T.es[16 * q:16 * q + 1, 0:MX])
+
+    tt = V([hop], v.transpose, T.tt[:], T.it[:])
+    off = V([tt, pm], v.tensor_copy, T.off[:], T.tt[:].indirect(T.pm[:]))
+
+    mm, have = [], [off, own, carr] + kl
+    for i in range(NP):
+        a, b, o = PW * i, PW * i + PW, T.off[:, PW // 16 * i:PW // 16 * (i + 1)]
+        t = V(have, v.tensor_copy, T.aftq[:, a:b].bitcast(u32), T.winq[:].bitcast(u32).indirect(o))
+        pl = S(have, T.afts[:, a:b], T.wins[:].indirect(o), ACT.Copy)
+        mm.append(P([t, pl, wq] + [sc[k] for k in range(8)], T.py[:, 512 * i:512 * i + PW], T.wq[:], T.wsc[:], T.aftq[:, a:b], T.afts[:, a:b], True, True))
+        D("y", [t], "sto", T.oc[:, 4 * a:4 * b], T.aftq[:, a:b].bitcast(u8))
+
+    def y_out(i, on_v):
+        o, p = T.ysb[:, PW * i:PW * i + PW], T.py[:, 512 * i:512 * i + PW]
+        t = V([mm[i]], v.tensor_copy, o, p) if on_v else S([mm[i]], o, p, ACT.Copy)
+        D("y", [t], "sto", T.y[:, PW * i:PW * i + PW], o)
+
+    y_out(0, True)
+    y_out(1, True)
+    y_out(2, False)
+    y_out(3, False)
+    for k in range(4):
+        D("y", [pl], "sto", T.osc[4 * k:4 * k + 4, :], T.afts[32 * k:32 * k + 4, :])
+
+    e0 = V([evx], v.tensor_tensor, T.e0[0:32, :], T.er[0:32, 0:64], T.er[0:32, 64:128], ALU.add)
+    e1 = V([e0], v.tensor_tensor, T.e1[0:32, :], T.e0[0:32, 0:32], T.e0[0:32, 32:64], ALU.add)
+    e2 = V([e1], v.tensor_tensor, T.e2[0:32, :], T.e1[0:32, 0:16], T.e1[0:32, 16:32], ALU.add)
+    e3 = V([e2], v.tensor_tensor, T.e3[0:32, :], T.e2[0:32, :], T.em[0:32, :], ALU.mult)
+    e4 = V([e3, eg], v.tensor_tensor, T.e4[0:32, :], T.e3[0:32, :], T.eg[0:32, :], ALU.add)
+    D("s", [e4], "sto", T.ev[:], T.e4[0:32, :])
+
+    for name in SEMAPHORES:
+        if name in total:
+            wait("g", [(name, total[name])])

@@ -4,31 +4,38 @@ from concourse.mybir import dt, AluOpType as ALU, ActivationFunctionType as ACT
 NR, NT, NC, CAP, MX = 4, 512, 1024, 96, 256
 NW = NC + NR * CAP
 LC = CAP // 16
-BLK = [3, 7, 2, 6, 1, 5, 0, 4]
-NS = 3
-VP, SP = [[4, 6], [3, 5, 7]], [[0, 2], [1]]
 WD = NC + 128
+HW = WD // 2
 TINY = 2.0 ** -120
-NP, PW = 4, 256
-UC = 14
+UC = 6
+SB = (0, 3, 4, 7)
+LISTS = ((0, 4), (4, 8))
+PIECES = ((0, 256), (256, 512), (512, 832), (832, 1024))
+ORDER = """
+col0 dif3a msk3 xq pq eq2 dif0a eq1 cmp1a col1 ps cmp2a eq6 sgn3a fl snd msk0 dif4a incl cmp6a sgn0a tie1 kb cmp2b cs x2 dif0b cmp5b sl
+dif3b cmp5a sgn0b num b2 xr cmp1b sgn3b sum2 join0 dif4b sum1 dd join3 pb eq5 dif7b gg0 dif7a msk4 cmp6b rk0 tie5 pt0 wq uu0 msk7 tr0 rn0
+sum5 c30 sum6 sgn4a ev0 sgn4b join4 sgn7b sgn7a ps0 pv0 pv1 join7 rk1 mm0 gg1 pt1 ps1 uu1 mm1 tr1 y0 rn1 y1 c31 ps2 ev1 pv2 et ps3 mm2 pv3
+l1 l2 osc l3 y2 mm3 l4 y3 evo
+"""
 
-SCRATCH = {"psv": ("psum", [128, 1024], "float32"), "pss": ("psum", [128, 1024], "float32"), "py": ("psum", [128, 2048], "float32")}
+SCRATCH = {"psv": ("psum", [128, 1024], "float32"), "pss": ("psum", [128, 1024], "float32"), "py": ("psum", [128, 2048], "float32"),
+           "tt": ("sbuf", [128, 32, 32], "float16"), "et": ("sbuf", [128, 8, 32], "float32")}
 _SPEC = {
-    "float8_e4m3fn_x4": "uq 144 urq 128 xq 512 wq 128 sndq 384 winq 1408 aftq 1024",
-    "uint8": "us 144 urs 128 xs 512 wsc 128 snds 384 wins 1408 afts 1024",
-    "int32": "sn8 24 ll 24 pi 8 pa 2 vo0 8 kk0 16 kk1 16",
-    "uint16": "su 24 lu 24 ul 8 rkd 16 rkn 8 off 64 vo 8 pm 4",
-    "bfloat16": "u0 16 ua 576 xt 2048 wt 512 eq 1024 eqm 384 w01 528 fl 384 incl 384 csg 768 cm3 1152 cm4 1152 cm5 1152 cm6 1152 cm7 1152 sg0 1024 sg1 1024 sg2 1024",
-    "float16": "co 192 scn 4608",
-    "float32": "df0 1024 df1 1024 df2 1024 scol 8 acc1 4 acc2 4 base 4 csum 2 ksl 2 kfl 2 a2 64 b2 64 "
-               "pos 264 pt 256 it 64 tt 64 ysb 1024 pf 2 kcol 2 kcoh 2 js 256 vj 128 vs 128 pm0 4 kk 16 "
-               "sr 1024 ej 1024 es 1024 er 128 e0 64 e1 32 e2 16 e3 16 e4 16 em 16 eg 16",
+    "float8_e4m3fn_x4": "uq 134 urq 128 xq 512 wq 128 sndq 384 winq 1408 aftq 1024",
+    "uint8": "us 134 urs 128 xs 512 wsc 128 snds 384 wins 1408 afts 1024",
+    "int32": "sn8 24 vo0 8",
+    "uint16": "su 24 lf 24 lu 24 ul 8 rkd 16 rkn 16 off 64 vo 8",
+    "bfloat16": "ua 536 xt 2048 wt 512 eq 1024 eqs 1024 tri 384 w01 16 fl 384 incl 384 csg 768 "
+                + " ".join("sg%d 1152" % i if i in SB else "cm%d 1024" % i for i in range(8)),
+    "float16": "scn 4096 pt 256",
+    "float32": "acc1 8 acc2 8 csum 2 a2 64 b2 64 tb 264 ysb 1024 kn 2 kb 2 ma 2 js 256 xx 256 xr 256 dd 128 "
+               "ee 1280 gg 8 uu 8 l1 16 l2 16 l3 32 l4 32 " + " ".join("df%d 1152" % i for i in SB),
 }
 for _d in _SPEC:
     _w = _SPEC[_d].split()
     for _i in range(0, len(_w), 2):
         SCRATCH[_w[_i]] = ("sbuf", [128, int(_w[_i + 1])], _d)
-SEMAPHORES = "qv qs qt qg lsn lu0 lk0 lk1 lk2 lx lw lown own hop evx sto larr carr sent".split()
+SEMAPHORES = "qv qs qt qg lsn lu0 lk0 lk1 lx lw own sto larr carr sent".split()
 
 
 def rank_program(g, core, T, topo):
@@ -64,27 +71,39 @@ def rank_program(g, core, T, topo):
     def D(q, deps, sem, out, in_):
         wait(q, deps); queues[q].dma_start(out, in_).then_inc(T.sem[sem], 16); return tick(sem, 16)
 
+    for q in range(2):
+        sn = D("ys"[q], [], "lsn", T.sn8[16 * q:16 * q + 16, :], T.sn[:])
+    u0 = D("y", [], "lu0", T.ua[:, 4 * UC:4 * UC + 16], T.u[:, 0:16])
     kl = []
-    for i, (a, b) in enumerate(((0, 256), (256, 512), (512, 1024))):
-        D("y", [], "lk%d" % i, T.winq[:, a:b].bitcast(u8), T.kc[:, 4 * a:4 * b])
-        kl.append(D("y", [], "lk%d" % i, T.wins[:, a:b], T.ks[:, a:b]))
-    u0 = D("s", [], "lu0", T.u0[:], T.u[:, 0:16])
-    for q in range(8):
-        sn = D("s" if q < 6 else "y", [], "lsn", T.sn8[16 * q:16 * q + 16, :], T.sn[:])
-    xl = D("y", [], "lx", T.xt[:], T.x[:])
+    for h in range(2):
+        a, b = 512 * h, 512 * h + 512
+        D("y", [], "lk%d" % h, T.winq[:, a:b].bitcast(u8), T.kc[:, 4 * a:4 * b])
+        kl.append(D("y", [], "lk%d" % h, T.wins[:, a:b], T.ks[:, a:b]))
+        if h == 0:
+            xl = D("y", [], "lx", T.xt[:], T.x[:])
     wl = D("y", [], "lw", T.wt[:], T.w[:])
 
-    G([], g.iota, T.pi[:, 0:4], [[0, 4]], 0, 1)
-    c_p = G([], g.iota, T.pi[:, 4:8], [[0, 4]], 0, 4)
-    c_pm = G([], g.iota, T.pm0[:], [[32, 2], [-2, 2]], 3, 0, **FL)
-    c_kk = G([], g.iota, T.kk0[0:32, :], [[1, 16]], 0, 16)
+    V([], v.memset, T.ua[:, 0:4 * UC], 0.0)
+    z_u = V([], v.memset, T.ua[:, 4 * UC + 16:], 0.0)
+    z_l = V([], v.memset, T.ul[:], UC)
+    V([], v.memset, T.w01[:, 0:1], 0.0)
+    z_w = V([], v.memset, T.w01[:, 1:16], 2.0)
+    zero = T.ua[:, 64:320]
+    z_x = S([z_u], T.xx[:], zero, ACT.Copy)
+    z_e = S([], T.ee[:, 0:MX], zero, ACT.Copy)
+    z_a = S([], T.a2[:], T.ua[:, 64:128], ACT.Copy)
+    z_t = S([], T.tb[:, 0:1], T.ua[:, 64:65], ACT.Copy)
+    z_3 = S([], T.l3[0:32, :], T.ua[0:32, 64:96], ACT.Copy)
     for a in range(4):
-        c_k = G([], g.iota, T.kcol[32 * a:32 * a + 32, :], [[32, 2]], 64 * a, 1, **FL)
-    c_vo = G([], g.iota, T.vo0[:], [[-128, 4], [512, 2]], 384, 1)
-    for b in range(4):
-        c_js = G([], g.iota, T.js[:, 64 * b:64 * b + 64], [[512, 2], [0, 2], [1, 16]], 384 - 128 * b, 1, **FL)
-    c_vj = G([], g.iota, T.vj[:], [[-128, 4], [512, 2], [1, 16]], 384, 1, **FL)
+        c_k = G([], g.iota, T.kn[32 * a:32 * a + 32, :], [[-64, 2]], -1 - 128 * a, -2, **FL)
+    c_vo = G([], g.iota, T.vo0[:], [[32, 8]], 0, 1)
 
+    for a in range(1, 4):
+        s8 = V([sn], v.tensor_copy, T.sn8[32 * a:32 * a + 32, :], T.sn8[0:32, :])
+    uq = V([u0, z_u], v.quantize_mx, T.uq[:], T.us[:], T.ua[:])
+    lf = V([s8], v.tensor_scalar, T.lf[:], T.sn8[:], 1.0, 1.0, ALU.add, ALU.min)
+    ur = V([uq, z_l], v.tensor_copy, T.urq[:].bitcast(u32), T.uq[:].bitcast(u32).indirect(T.ul[:]))
+    us = S([uq, z_l], T.urs[:], T.us[:].indirect(T.ul[:]), ACT.Copy)
     others = [d for d in range(NR) if d != me]
     emask = {d: sum(1 << e for e in topo.engines(core, T.cores[d])[2 * i:2 * i + 2]) for i, d in enumerate(others)}
 
@@ -98,204 +117,233 @@ def rank_program(g, core, T, topo):
         g.remote_dma_fused(tr, local_sem=T.sem.sent)
         tick("sent", 2 * len(others))
 
-    send([sn], "larr", lambda d: T.sn8[:, LC * d:LC * d + LC], lambda d: T.ll[:, LC * me:LC * me + LC])
+    send([lf], "larr", lambda d: T.lf[:, LC * d:LC * d + LC], lambda d: T.lu[:, LC * me:LC * me + LC])
     larr = tick("larr", 2 * len(others))
-    lown = D("y", [sn], "lown", T.ll[:, LC * me:LC * me + LC], T.sn8[:, LC * me:LC * me + LC])
+    fl0 = S([lf, z_w], T.fl[:, CAP * me:CAP * me + CAP], T.w01[:].indirect(T.lf[:, LC * me:LC * me + LC]), ACT.Copy)
+    c_t = G([z_u], g.affine_select, T.tri[:], T.ua[:, 64:448], [[0, 3], [-1, 128]], ALU.is_ge, 1.0, 0, 1)
+    su = V([], v.tensor_copy, T.su[:], T.sn8[:])
+    for a in range(4):
+        vo = V([c_vo], v.tensor_copy, T.vo[32 * a:32 * a + 32, :], T.vo0[0:32, :])
+    z_m = V([z_e], v.memset, T.ee[0:1, 0:MX], -1.0)
 
-    z_u = V([], v.memset, T.ua[:], 0.0)
-    z_l = V([], v.memset, T.ul[:], UC)
-    t = V([u0, z_u], v.tensor_copy, T.ua[:, 4 * UC:4 * UC + 4], T.u0[:, 0:4])
-    uq = V([t], v.quantize_mx, T.uq[:], T.us[:], T.ua[:])
-    ur = V([uq, z_l], v.tensor_copy, T.urq[:].bitcast(u32), T.uq[:].bitcast(u32).indirect(T.ul[:]))
-    S([z_u], T.w01[:, 1:513], T.ua[:, 64:576], ACT.Identity, bias=1.0, scale=0.0)
-    us = S([uq, z_l], T.urs[:], T.us[:].indirect(T.ul[:]), ACT.Copy)
-    z2 = S([], T.w01[:, 0:1], T.ua[:, 64:65], ACT.Copy)
-    z3 = S([], T.a2[:], T.ua[:, 64:128], ACT.Copy)
-    z8 = S([], T.pos[:, MX:MX + 8], T.ua[:, 64:72], ACT.Copy)
-    V([c_p], v.tensor_scalar, T.pa[:, 0:1], T.pi[:, 4:5], 28, None, ALU.bitwise_and)
-    a2 = V([], v.tensor_scalar, T.pa[:, 1:2], T.pi[:, 0:1], 3, 1, ALU.logical_shift_right, ALU.bitwise_and)
-    f7 = V([], v.tensor_scalar, T.pf[:, 1:2], T.pi[:, 0:1], 16, None, ALU.is_lt)
-    f6 = V([a2], v.tensor_tensor, T.pf[:, 0:1], T.pa[:, 0:1], T.pa[:, 1:2], ALU.subtract)
-    kk1 = V([c_kk], v.tensor_scalar, T.kk1[0:32, :], T.kk0[0:32, :], MX - 1, None, ALU.bitwise_and)
-    pm = V([f6, c_pm], v.tensor_scalar, T.pm[:], T.pm0[:], T.pf[:, 0:1], None, ALU.add)
-    kk = V([kk1], v.tensor_copy, T.kk[0:32, :], T.kk1[0:32, :])
-    kc = V([c_k], v.tensor_scalar, T.kcoh[:], T.kcol[:], 0.5, None, ALU.add)
-
-    def rows(ps, h):
+    rv, rs, pc = [], [], []
+    for h in range(2):
         a, b = 512 * h, 512 * h + 512
-        return P([ur, us, kl[h + 1]], ps[:, a:b], T.urq[:], T.urs[:], T.winq[:, a:b], T.wins[:, a:b], True, True)
+        for i in range(4):
+            c, o = a + 128 * i, UC - 2 * i
+            t = P([uq, kl[h]], T.py[:, a:a + 128], T.winq[:, c:c + 128], T.wins[:, c:c + 128], T.uq[:, o:o + 128], T.us[:, o:o + 128], i == 0, i == 3)
+        pc.append(t)
+        for ps, r in ((T.psv, rv), (T.pss, rs))[::2 * h - 1]:
+            r.append(P([ur, us], ps[:, a:b], T.urq[:], T.urs[:], T.winq[:, a:b], T.wins[:, a:b], True, True))
 
-    sc = {}
+    R = {}
+    w0, own0, m2 = NC + CAP * me, CAP * me, T.incl[:, NR * CAP - 1:NR * CAP]
 
-    def cols(bank, places, dep):
-        for i in places:
-            b, o = 128 * BLK[i], UC - 2 * i
-            sc[i] = P([uq, dep], T.py[:, 512 * bank:512 * bank + 128], T.winq[:, b:b + 128], T.wins[:, b:b + 128],
-                      T.uq[:, o:o + 128], T.us[:, o:o + 128], i == places[0], i == places[-1])
+    def own_score(i):
+        return T.xx[:, 32 * i + 1:32 * i + 2]
 
-    rv, rs = [], []
-    cols(0, VP[0], kl[0])
-    rv.append(rows(T.psv, 0))
-    cols(1, SP[0], kl[1])
-    rs.append(rows(T.pss, 0))
-    cols(2, VP[1], kl[2])
-    rv.append(rows(T.psv, 1))
-    cols(3, SP[1], kl[2])
-    rs.append(rows(T.pss, 1))
+    def runs(h, cut):
+        a, b = 512 * h, 512 * h + 512
+        m = min(max(cut, a), b)
+        return [(lo, hi, k) for k, (lo, hi) in enumerate(((a, m), (m, b))) if lo < hi]
 
-    def columns(h, on_v):
-        places, bank = (VP if on_v else SP)[h], 512 * (2 * h + (not on_v))
-        i, j = places[0], places[-1] + 1
-        o, p, d = T.scol[:, i:j:2], T.py[:, bank + 2 * i:bank + 2 * j:4], [sc[places[-1]]]
-        t = V(d, v.tensor_copy, o, p) if on_v else S(d, o, p, ACT.Copy)
-        for k in places:
-            sc[k] = t
+    def vrun(i):
+        j = i
+        while j < 8 and j not in SB:
+            j += 1
+        return range(i, j)
 
-    def s_diff(i, a, b):
-        return S([rs[a // 512], rs[(b - 1) // 512], sc[i]], T["df%d" % i][:, a:b], T.pss[:, a:b], ACT.Identity, bias=T.scol[:, i:i + 1], scale=-1.0)
+    def tie_of(i):
+        return [R["tie%d" % k] for k in range(8) if "tie%d" % k in R and i in vrun(k)]
 
-    def s_sign(i, d):
-        b, df, sg = 128 * BLK[i], T["df%d" % i], T["sg%d" % i]
-        S([d], sg[:, 0:b], df[:, 0:b], ACT.Sign, bias=TINY, accum_out=T.acc1[:, i:i + 1])
-        return S([d], sg[:, b:NC], df[:, b:NC], ACT.Sign, bias=-TINY, accum_out=T.acc2[:, i:i + 1])
+    def count(k):
+        a, b = LISTS[k]
+        return T.scn[:, 512 * a + 511:512 * b:512], [R["join%d" % i if i in SB else "sum%d" % i] for i in range(a, b)]
 
-    def v_cmp(i, a, b):
-        m, cm, t = min(max(128 * BLK[i], a), b), T["cm%d" % i], None
-        for lo, hi, op in ((a, m, ALU.is_le), (m, b, ALU.is_lt)):
-            if lo < hi:
-                t = V([rv[lo // 512], rv[(hi - 1) // 512], sc[i]], v.tensor_scalar, cm[:, lo:hi], T.psv[:, lo:hi], T.scol[:, i:i + 1], 2.0, op, ALU.mult)
+    def col(h):
+        return V([pc[h], z_x], v.tensor_copy, T.xx[:, 128 * h + 1:128 * h + 128:32], T.py[:, 512 * h:512 * h + 8:2])
+
+    def dif(i, h):
+        for lo, hi, k in runs(h, 128 * i + 128 * (i % 4 == 3)):
+            t = S([rs[h], R["col%d" % (i // 4)]], T["df%d" % i][:, lo + 128 * k:hi + 128 * k], T.pss[:, lo:hi], ACT.Identity, bias=own_score(i), scale=-1.0)
         return t
 
-    def v_sum(i, c):
-        cm, o = T["cm%d" % i], WD // 2 * i
-        return V([c, eqm[i]], v.tensor_tensor_scan, T.scn[:, o:o + WD // 2], cm[:, 0:WD // 2], cm[:, WD // 2:WD], 0.0, ALU.add, ALU.add)
+    def msk(i):
+        df, b, d = T["df%d" % i], 128 * i, [R["dif%d%s" % (i, "ab"[i // 4])]]
+        lo, hi = df[:, b:b + 128], df[:, b + 128:b + 256]
+        early = lambda src: G(d, g.affine_select, lo, src, [[-1, 128]], ALU.is_gt, -1.0, 0, 1)
+        late = lambda src: G(d, g.affine_select, hi, src, [[1, 128]], ALU.is_ge, -1.0, 0, -1)
+        if i % 4 == 3:
+            late(lo)
+            return early(lo)
+        early(hi)
+        return late(hi)
 
-    def v_eq(h, places):
-        for i in places:
-            b = 128 * BLK[i]
-            eqt[i] = V([sc[i], rv[h]], v.tensor_scalar, T.eq[:, 128 * i:128 * i + 128], T.psv[:, b:b + 128], T.scol[:, i:i + 1], 2.0, ALU.is_equal, ALU.mult)
+    def sgn(i, part):
+        b, df, sg = 128 * i + 128, T["df%d" % i], T["sg%d" % i]
+        if part == 0:
+            d = [R["dif%da" % i], R["msk%d" % i]] + ([R["dif%db" % i]] if i > 4 else [])
+            return S(d, sg[:, 0:b], df[:, 0:b], ACT.Sign, bias=-TINY, scale=-1.0, accum_out=T.acc1[:, i:i + 1])
+        d = [R["dif%da" % i], R["dif%db" % i], R["msk%d" % i]]
+        return S(d, sg[:, b:WD], df[:, b:WD], ACT.Sign, bias=TINY, scale=-1.0, accum_out=T.acc2[:, i:i + 1])
 
-    def g_eq(i):
-        eqm[i] = G([eqt[i]], g.affine_select, T["cm%d" % i][:, NC:WD], T.eq[:, 128 * i:128 * i + 128], [[-1, 128]], ALU.is_gt, 0.0, 0, 1)
+    def join(i):
+        o = 512 * i + 511
+        return V([R["sgn%da" % i], R["sgn%db" % i]], v.tensor_scalar, T.scn[:, o:o + 1], T.acc1[:, i:i + 1], T.acc2[:, i:i + 1], 0.5, ALU.add, ALU.mult)
 
-    eqt, eqm = {}, {}
-    columns(0, True)
-    columns(0, False)
-    s_diff(0, 0, 512)
-    v_eq(0, VP[0])
-    s_diff(2, 0, 512)
-    for i in VP[0]:
-        g_eq(i)
-    v_cmp(4, 0, 512)
-    v_cmp(6, 0, 512)
-    v_eq(0, SP[0])
-    su = V([sn], v.tensor_copy, T.su[:], T.sn8[:])
-    columns(1, True)
-    columns(1, False)
-    v_eq(1, VP[1])
-    for i in VP[1]:
-        g_eq(i)
-    d0 = s_diff(0, 512, 1024)
-    s_sign(0, d0)
-    c4 = v_cmp(4, 512, 1024)
-    v_eq(1, SP[1])
-    eqs = G([eqt[1]], g.affine_select, T.eqm[:], T.eq[:, 0:128 * NS], [[0, NS], [-1, 128]], ALU.is_gt, 0.0, 0, 1)
-    xq = V([xl], v.quantize_mx, T.xq[:], T.xs[:], T.xt[:])
-    c6 = v_cmp(6, 512, 1024)
-    pq = V([xq, su], v.tensor_copy, T.sndq[:].bitcast(u32), T.xq[:].bitcast(u32).indirect(T.su[:]))
-    ps = S([xq, su], T.snds[:], T.xs[:].indirect(T.su[:]), ACT.Copy)
-    w0, own0 = NC + CAP * me, CAP * me
-    send([pq], "carr", lambda d: T.sndq[:, CAP * d:CAP * d + CAP].bitcast(u8), lambda d: T.winq[:, w0:w0 + CAP].bitcast(u8))
-    send([ps], "carr", lambda d: T.snds[:, CAP * d:CAP * d + CAP], lambda d: T.wins[:, w0:w0 + CAP])
-    carr = tick("carr", 4 * len(others))
-    D("y", [pq], "own", T.winq[:, w0:w0 + CAP].bitcast(u8), T.sndq[:, own0:own0 + CAP].bitcast(u8))
-    own = D("y", [ps], "own", T.wins[:, w0:w0 + CAP], T.snds[:, own0:own0 + CAP])
-    z6 = G([], g.iota, T.ej[:, 0:MX], [[0, MX]], 0, 0, **FL)
-    z7 = G([], g.iota, T.es[:, 0:MX], [[0, MX]], 0, 0, **FL)
+    def cmp(i, h):
+        for lo, hi, k in runs(h, 128 * i + 128):
+            t = V([rv[h], R["col%d" % (i // 4)]], v.tensor_scalar, T["cm%d" % i][:, lo:hi], T.psv[:, lo:hi], own_score(i), HW / NC - 1.0,
+                  (ALU.is_gt, ALU.is_ge)[k], ALU.add)
+        return t
 
-    v_sum(4, c4)
-    d2 = s_diff(2, 512, 1024)
-    lu = V([larr, lown], v.tensor_scalar, T.lu[:], T.ll[:], 1.0, None, ALU.add)
-    fl = S([lu, z2], T.fl[:], T.w01[:].indirect(T.lu[:]), ACT.Copy)
-    s_sign(2, d2)
-    c3 = v_cmp(3, 0, 1024)
-    v_sum(6, c6)
-    incl = V([fl], v.tensor_tensor_scan, T.incl[:], T.fl[:], T.fl[:], 0.0, ALU.add, ALU.max)
-    for h in range(2):
-        cs = S([incl, kc], T.csg[:, 384 * h:384 * h + 384], T.incl[:], ACT.Sign, bias=T.kcoh[:, h:h + 1], scale=-1.0, accum_out=T.csum[:, h:h + 1])
-    d1 = s_diff(1, 0, 1024)
-    c5 = v_cmp(5, 0, 1024)
-    sg = s_sign(1, d1)
-    v_sum(3, c3)
-    co, n64 = {}, float(NC)
-    for i in range(NS):
-        a = 128 * i
-        co[i] = V([eqs], v.tensor_tensor_scan, T.co[:, 64 * i:64 * i + 64], T.eqm[:, a:a + 64], T.eqm[:, a + 64:a + 128], n64, ALU.add, ALU.add)
-        if i == 0:
-            sl = V([cs], v.tensor_scalar, T.ksl[:], T.csum[:], 0.5, float(NC + NR * CAP // 2), ALU.mult, ALU.add)
-        if i == 1:
-            kf = V([sl], v.tensor_scalar, T.kfl[:], T.ksl[:], float(NW), None, ALU.is_lt)
-    km = V([kf, z3], v.tensor_tensor, T.a2[:, 0:64:32], T.ksl[:], T.kfl[:], ALU.mult)
-    v_sum(5, c5)
-    b2 = V([km], v.transpose, T.b2[:], T.a2[:])
-    for a in range(4):
-        pos = G([b2], g.partition_broadcast, T.pos[:, 64 * a:64 * a + 64], T.b2[32 * a:32 * a + 1, :], 128)
-    c7 = v_cmp(7, 0, 1024)
-    sm = v_sum(7, c7)
-    last, step = WD // 2 - 1, WD // 2
-    bs = V([sg, co[NS - 1]], v.tensor_tensor, T.base[:, 0:NS], T.co[:, 63:64 * NS:64], T.acc1[:, 0:NS], ALU.add)
-    cn = V([bs], v.tensor_tensor, T.scn[:, last:NS * step:step], T.base[:, 0:NS], T.acc2[:, 0:NS], ALU.add)
-    cnt = T.scn[:, last:8 * step:step]
+    def eq(i):
+        b = 128 * i
+        return V([R["col%d" % (i // 4)], rv[i // 4]], v.tensor_scalar, T.eq[:, b:b + 128], T.psv[:, b:b + 128], own_score(i), None, ALU.is_equal)
 
-    V([cn, sm], v.tensor_scalar, T.rkd[:, 0:16:2], cnt, 0.5, float(MX), ALU.mult, ALU.min)
-    rd = V([], v.tensor_scalar, T.rkd[:, 1:16:2], cnt, 0.5, float(MX), ALU.mult, ALU.min)
-    rn = V([], v.tensor_scalar, T.rkn[:], cnt, 0.5, None, ALU.mult)
-    pt = V([rd, pos, z8, c_js], v.tensor_tensor, T.pt[:], T.pos[:].indirect(T.rkd[:]), T.js[:], ALU.max)
-    for a in range(4):
-        hop = D("y", [pt], "hop", T.it[32 * a:32 * a + 32, :], T.pt[0:128:16, :])
+    def tie(i):
+        a, b = 128 * i, 128 * vrun(i)[-1] + 128
+        return V([R["eq%d" % k] for k in vrun(i)] + [c_t], v.tensor_tensor_scan, T.eqs[:, a:b], T.tri[:, 0:b - a], T.eq[:, a:b], 0.0, ALU.mult, ALU.add)
 
-    vo = V([c_vo], v.tensor_copy, T.vo[:], T.vo0[:])
-    sr = S([], T.sr[:], T.pss[:], ACT.Copy)
-    vs = S([sr, vo], T.vs[:], T.sr[:].indirect(T.vo[:]), ACT.Copy)
-    em = V([kk, incl], v.tensor_scalar, T.em[0:32, :], T.kk[0:32, :], T.incl[0:32, NR * CAP - 1:NR * CAP], None, ALU.is_lt)
-    ej = V([rn, z6, c_vj], v.tensor_copy, T.ej[:].indirect(T.rkn[:]), T.vj[:])
-    for q in range(8):
-        D("s", [ej], "evx", T.er[0:16, 16 * q:16 * q + 16], T.ej[16 * q:16 * q + 1, 0:MX])
-    wq = V([wl], v.quantize_mx, T.wq[:], T.wsc[:], T.wt[:])
-    eg = V([em, f7], v.tensor_scalar, T.eg[0:32, :], T.em[0:32, :], -1.0, T.pf[0:32, 1:2], ALU.add, ALU.mult)
-    es = V([vs, z7], v.tensor_copy, T.es[:].indirect(T.rkn[:]), T.vs[:])
-    for q in range(8):
-        evx = D("y", [es], "evx", T.er[16:32, 16 * q:16 * q + 16], T.es[16 * q:16 * q + 1, 0:MX])
+    def vsum(i):
+        cm, o, e = T["cm%d" % i], 512 * i, 128 * i + 127
+        return V([R["cmp%da" % i], R["cmp%db" % i]] + tie_of(i), v.tensor_tensor_scan, T.scn[:, o:o + 512], cm[:, 0:512], cm[:, 512:NC],
+                 T.eqs[:, e:e + 1], ALU.add, ALU.add)
 
-    tt = V([hop], v.transpose, T.tt[:], T.it[:])
-    off = V([tt, pm], v.tensor_copy, T.off[:], T.tt[:].indirect(T.pm[:]))
+    def snd():
+        send([R["pq"]], "carr", lambda d: T.sndq[:, CAP * d:CAP * d + CAP].bitcast(u8), lambda d: T.winq[:, w0:w0 + CAP].bitcast(u8))
+        send([R["ps"]], "carr", lambda d: T.snds[:, CAP * d:CAP * d + CAP], lambda d: T.wins[:, w0:w0 + CAP])
+        D("y", [R["pq"]], "own", T.winq[:, w0:w0 + CAP].bitcast(u8), T.sndq[:, own0:own0 + CAP].bitcast(u8))
+        R["own"] = D("y", [R["ps"]], "own", T.wins[:, w0:w0 + CAP], T.snds[:, own0:own0 + CAP])
+        return tick("carr", 4 * len(others))
 
-    mm, have = [], [off, own, carr] + kl
-    for i in range(NP):
-        a, b, o = PW * i, PW * i + PW, T.off[:, PW // 16 * i:PW // 16 * (i + 1)]
-        t = V(have, v.tensor_copy, T.aftq[:, a:b].bitcast(u32), T.winq[:].bitcast(u32).indirect(o))
-        pl = S(have, T.afts[:, a:b], T.wins[:].indirect(o), ACT.Copy)
-        mm.append(P([t, pl, wq] + [sc[k] for k in range(8)], T.py[:, 512 * i:512 * i + PW], T.wq[:], T.wsc[:], T.aftq[:, a:b], T.afts[:, a:b], True, True))
+    def fl():
+        t = fl0
+        for a, b in ((0, LC * me), (LC * me + LC, LC * NR)):
+            if a < b:
+                t = S([larr], T.fl[:, 16 * a:16 * b], T.w01[:].indirect(T.lu[:, a:b]), ACT.Copy)
+        return t
+
+    def kb():
+        t = S([R["incl"], c_k], T.kb[:], T.kn[:], ACT.Identity, bias=m2)
+        S([], T.ma[:, 0:1], m2, ACT.Identity, bias=-float(HW), scale=0.5)
+        R["ma"] = S([], T.ma[:, 1:2], m2, ACT.Identity, bias=float(HW), scale=-0.5)
+        return t
+
+    def cs():
+        for h in range(2):
+            t = S([R["kb"]], T.csg[:, 384 * h:384 * h + 384], T.incl[:], ACT.Sign, bias=T.kb[:, h:h + 1], scale=-1.0, accum_out=T.csum[:, h:h + 1])
+        return t
+
+    def pb():
+        for a in range(4):
+            t = G([R["b2"]], g.partition_broadcast, T.tb[:, 1 + 64 * a:65 + 64 * a], T.b2[32 * a:32 * a + 1, :], 128)
+        return t
+
+    def num():
+        R["js"] = G([], g.iota, T.js[:], [[128, 8], [0, 2], [1, 16]], 0, 1, **FL)
+        G([z_x], g.iota, T.xx[:, 0:256:16], [[128, 8], [0, 2]], 1, 1, **FL)
+        return G([], g.iota, T.xx[0:16, 0:256:16], [[128, 8], [0, 2]], 0, 1, **FL)
+
+    def rk(k):
+        (a, b), (cnt, d) = LISTS[k], count(k)
+        for e in range(2):
+            t = V(d + [R["ma"]], v.tensor_scalar, T.rkd[:, 2 * a + e:2 * b:2], cnt, T.ma[:, 0:1], 0.0, ALU.add, ALU.max)
+        return t
+
+    def pt(k):
+        a, b = LISTS[k]
+        return V([R["rk%d" % k], R["pb"], z_t, R["js"]], v.tensor_tensor, T.pt[:, 32 * a:32 * b], T.tb[:].indirect(T.rkd[:, 2 * a:2 * b]),
+                 T.js[:, 32 * a:32 * b], ALU.max)
+
+    def tr(k):
+        a, b = LISTS[k]
+        for q in range(4):
+            t = V([R["pt%d" % k]], v.transpose, T.tt[0:32, 4 * a + q:4 * b:4, :], T.pt[32 * q:32 * q + 32, 32 * a:32 * b])
+        return t
+
+    def c3(k):
+        a, b = LISTS[k]
+        for q in range(4):
+            t = V([R["tr%d" % k]], v.tensor_copy, T.off[32 * q:32 * q + 32, 8 * a:8 * b], T.tt[0:32, 4 * a:4 * b, 0:32:16])
+        return t
+
+    def gg(k):
+        (a, b), (cnt, d) = LISTS[k], count(k)
+        return V(d + [R["ma"]], v.tensor_scalar, T.gg[:, a:b], cnt, T.ma[:, 1:2], float(MX), ALU.is_le, ALU.mult)
+
+    def uu(k):
+        (a, b), (cnt, d) = LISTS[k], count(k)
+        return V([R["gg%d" % k]], v.tensor_tensor, T.uu[:, a:b], T.gg[:, a:b], cnt, ALU.subtract)
+
+    def rn(k):
+        a, b = LISTS[k]
+        return V([R["uu%d" % k]], v.tensor_scalar, T.rkn[:, 8 * k:8 * k + b - a], T.uu[:, a:b], float(HW), None, ALU.add)
+
+    def ev(k):
+        a, b = LISTS[k]
+        return V([R["rn%d" % k], z_m, R["dd"]] + ([R["ev0"]] if k else []), v.tensor_copy, T.ee[:].indirect(T.rkn[:, 8 * k:8 * k + b - a]), T.dd[:, 16 * a:16 * b])
+
+    def have(i):
+        return [R["c3%d" % (i // 2)], R["own"], R["snd"]] + kl
+
+    def pv(i):
+        a, b = PIECES[i]
+        t = V(have(i), v.tensor_copy, T.aftq[:, a:b].bitcast(u32), T.winq[:].bitcast(u32).indirect(T.off[:, a // 16:b // 16]))
         D("y", [t], "sto", T.oc[:, 4 * a:4 * b], T.aftq[:, a:b].bitcast(u8))
+        return t
 
-    def y_out(i, on_v):
-        o, p = T.ysb[:, PW * i:PW * i + PW], T.py[:, 512 * i:512 * i + PW]
-        t = V([mm[i]], v.tensor_copy, o, p) if on_v else S([mm[i]], o, p, ACT.Copy)
-        D("y", [t], "sto", T.y[:, PW * i:PW * i + PW], o)
+    def psc(i):
+        a, b = PIECES[i]
+        return S(have(i), T.afts[:, a:b], T.wins[:].indirect(T.off[:, a // 16:b // 16]), ACT.Copy)
 
-    y_out(0, True)
-    y_out(1, True)
-    y_out(2, False)
-    y_out(3, False)
-    for k in range(4):
-        D("y", [pl], "sto", T.osc[4 * k:4 * k + 4, :], T.afts[32 * k:32 * k + 4, :])
+    def mm(i):
+        a, b = PIECES[i]
+        return P([R["pv%d" % i], R["ps%d" % i], R["wq"], R["col0"], R["col1"]], T.py[:, 512 * i:512 * i + b - a], T.wq[:], T.wsc[:],
+                 T.aftq[:, a:b], T.afts[:, a:b], True, True)
 
-    e0 = V([evx], v.tensor_tensor, T.e0[0:32, :], T.er[0:32, 0:64], T.er[0:32, 64:128], ALU.add)
-    e1 = V([e0], v.tensor_tensor, T.e1[0:32, :], T.e0[0:32, 0:32], T.e0[0:32, 32:64], ALU.add)
-    e2 = V([e1], v.tensor_tensor, T.e2[0:32, :], T.e1[0:32, 0:16], T.e1[0:32, 16:32], ALU.add)
-    e3 = V([e2], v.tensor_tensor, T.e3[0:32, :], T.e2[0:32, :], T.em[0:32, :], ALU.mult)
-    e4 = V([e3, eg], v.tensor_tensor, T.e4[0:32, :], T.e3[0:32, :], T.eg[0:32, :], ALU.add)
-    D("s", [e4], "sto", T.ev[:], T.e4[0:32, :])
+    def y(i):
+        a, b = PIECES[i]
+        t = S([R["mm%d" % i]], T.ysb[:, a:b], T.py[:, 512 * i:512 * i + b - a], ACT.Copy)
+        return D("y", [t], "sto", T.y[:, a:b], T.ysb[:, a:b])
+
+    def osc():
+        for k in range(4):
+            D("y", [R["ps%d" % i] for i in range(4)], "sto", T.osc[4 * k:4 * k + 4, :], T.afts[32 * k:32 * k + 4, :])
+
+    def l1():
+        for e in range(2):
+            t = V([R["et"]], v.tensor_tensor, T.l1[:, 8 * e:8 * e + 8], T.et[:, :, e], T.et[:, :, 16 + e], ALU.add)
+        return t
+
+    plain = {
+        "xq": lambda: V([xl], v.quantize_mx, T.xq[:], T.xs[:], T.xt[:]),
+        "pq": lambda: V([R["xq"], su], v.tensor_copy, T.sndq[:].bitcast(u32), T.xq[:].bitcast(u32).indirect(T.su[:])),
+        "ps": lambda: S([R["xq"], su], T.snds[:], T.xs[:].indirect(T.su[:]), ACT.Copy),
+        "wq": lambda: V([wl], v.quantize_mx, T.wq[:], T.wsc[:], T.wt[:]),
+        "incl": lambda: V([R["fl"]], v.tensor_tensor_scan, T.incl[:], T.fl[:], T.fl[:], 0.0, ALU.add, ALU.max),
+        "sl": lambda: S([R["cs"], z_a], T.a2[:, 0:64:32], T.csum[:], ACT.Identity, bias=float(NC + NR * CAP // 2), scale=0.5),
+        "b2": lambda: V([R["sl"]], v.transpose, T.b2[:], T.a2[:]),
+        "x2": lambda: S([R["col0"], R["col1"]], T.xx[:, 17:256:32], T.xx[:, 1:256:32], ACT.Copy),
+        "xr": lambda: V([R["x2"], R["num"]], v.transpose, T.xr[:], T.xx[:]),
+        "dd": lambda: S([R["xr"], vo], T.dd[:], T.xr[:].indirect(T.vo[:]), ACT.Copy),
+        "et": lambda: V([R["ev1"]], v.transpose, T.et[:], T.ee[:, 0:MX]),
+        "l2": lambda: V([R["l1"]], v.tensor_tensor, T.l2[0:64, :], T.l1[0:64, :], T.l1[64:128, :], ALU.add),
+        "l3": lambda: V([R["l2"], z_3], v.tensor_tensor, T.l3[0:32, 0:16], T.l2[0:32, :], T.l2[32:64, :], ALU.add),
+        "l4": lambda: V([R["l3"]], v.transpose, T.l4[0:32, :], T.l3[0:32, :]),
+        "evo": lambda: D("s", [R["l4"]], "sto", T.ev[:], T.l4[0:16, :]),
+        "snd": snd, "fl": fl, "kb": kb, "cs": cs, "pb": pb, "num": num, "osc": osc, "l1": l1,
+    }
+    numbered = {"col": col, "msk": msk, "join": join, "eq": eq, "tie": tie, "sum": vsum, "rk": rk, "pt": pt, "tr": tr, "c3": c3,
+                "gg": gg, "uu": uu, "rn": rn, "ev": ev, "pv": pv, "ps": psc, "mm": mm, "y": y}
+    halved = {"dif": dif, "sgn": sgn, "cmp": cmp}
+    for name in ORDER.split():
+        if name in plain:
+            R[name] = plain[name]()
+        elif name[-1] in "ab":
+            R[name] = halved[name[:-2]](int(name[-2]), "ab".index(name[-1]))
+        else:
+            R[name] = numbered[name[:-1]](int(name[-1]))
 
     for name in SEMAPHORES:
         if name in total:

@@ -7,29 +7,31 @@ LC = CAP // 16
 WD = NC + 128
 HW = WD // 2
 TINY = 2.0 ** -120
-UC = 6
-SB = (0, 3, 4, 7)
-LISTS = ((0, 4), (4, 8))
-PIECES = ((0, 256), (256, 512), (512, 832), (832, 1024))
+UC = 12
+SB = (0, 3, 7)
+HALF = (6,)
+CG = ((0, 3), (1, 2), (4, 5, 6, 7))
+LISTS = ((0, 5), (5, 8))
+PIECES = ((0, 320), (320, 640), (640, 896), (896, 1024))
 ORDER = """
-col0 dif3a msk3 xq pq eq2 dif0a eq1 cmp1a col1 ps cmp2a eq6 sgn3a fl snd msk0 dif4a incl cmp6a sgn0a tie1 kb cmp2b cs x2 dif0b cmp5b sl
-dif3b cmp5a sgn0b num b2 xr cmp1b sgn3b sum2 join0 dif4b sum1 dd join3 pb eq5 dif7b gg0 dif7a msk4 cmp6b rk0 tie5 pt0 wq uu0 msk7 tr0 rn0
-sum5 c30 sum6 sgn4a ev0 sgn4b join4 sgn7b sgn7a ps0 pv0 pv1 join7 rk1 mm0 gg1 pt1 ps1 uu1 mm1 tr1 y0 rn1 y1 c31 ps2 ev1 pv2 et ps3 mm2 pv3
-l1 l2 osc l3 y2 mm3 l4 y3 evo
+col0! col1 dif3a xq dif0a cmp1a ps msk3 cmp2a eq1 eq2 msk0 sgn3a pq col2 tie1 cmp2b snd fl eq6 cmp1b num sgn0a dif3b incl sum2 dif7w
+kb! cmp4w cs msk7 cmp5w dif0b sl! sgn3b eq4 b2 eq5 pb cmp6b sgn0b join3 tie4 sum1 sum4 ma hd6 xr join0 wq sgn7b rk0 hs6 sum5 pt0 hj6
+gg0 sgn7a tr0 sum6 c30 uu0 pv0 ps0 join7 dd pv1 oc0 mm0 ps1 rk1 oc1 rn0 y0 gg1 mm1 pt1 uu1 ys0 y1 tr1 rn1 ys1 c31 ev0 ps3 ps2 pv3 pv2
+mm3 oc3 os3! os1 y3 ev1 os2! mm2 oc2 ys3 et y2 os0! l1 ys2 l2 l3 l4 eo0! eo1
 """
 
 SCRATCH = {"psv": ("psum", [128, 1024], "float32"), "pss": ("psum", [128, 1024], "float32"), "py": ("psum", [128, 2048], "float32"),
-           "tt": ("sbuf", [128, 32, 32], "float16"), "et": ("sbuf", [128, 8, 32], "float32")}
+           "tt": ("sbuf", [128, 32, 32], "float16"), "et": ("sbuf", [128, 8, 32], "float32"), "xx": ("sbuf", [128, 8, 32], "float32")}
 _SPEC = {
-    "float8_e4m3fn_x4": "uq 134 urq 128 xq 512 wq 128 sndq 384 winq 1408 aftq 1024",
-    "uint8": "us 134 urs 128 xs 512 wsc 128 snds 384 wins 1408 afts 1024",
+    "float8_e4m3fn_x4": "uq 142 urq 128 xq 512 wq 128 sndq 384 winq 1408 aftq 1024",
+    "uint8": "us 142 urs 128 xs 512 wsc 128 snds 384 wins 1408 afts 1024",
     "int32": "sn8 24 vo0 8",
-    "uint16": "su 24 lf 24 lu 24 ul 8 rkd 16 rkn 16 off 64 vo 8",
-    "bfloat16": "ua 536 xt 2048 wt 512 eq 1024 eqs 1024 tri 384 w01 16 fl 384 incl 384 csg 768 "
-                + " ".join("sg%d 1152" % i if i in SB else "cm%d 1024" % i for i in range(8)),
+    "uint16": "su 24 lf 24 lu 24 ul 8 rkd 16 rkn 24 off 64 vo 8",
+    "bfloat16": "ua 568 xt 2048 wt 512 eq 1024 eqs 1024 tri 384 w01 16 fl 384 incl 384 csg 768 "
+                + " ".join("sg%d 1152" % i if i in SB else "cm%d 1024" % i for i in range(8)) + "".join(" sh%d 512" % i for i in HALF),
     "float16": "scn 4096 pt 256",
-    "float32": "acc1 8 acc2 8 csum 2 a2 64 b2 64 tb 264 ysb 1024 kn 2 kb 2 ma 2 js 256 xx 256 xr 256 dd 128 "
-               "ee 1280 gg 8 uu 8 l1 16 l2 16 l3 32 l4 32 " + " ".join("df%d 1152" % i for i in SB),
+    "float32": "acc1 8 acc2 8 csum 2 a2 64 b2 64 tb 264 ysb 1024 kn 2 kb 2 ma 2 js 256 dum 1024 xr 256 dd 128 "
+               "ee 1280 gg 8 uu 8 l1 16 l2 16 l3 32 l4 32 " + " ".join("df%d 1152" % i for i in SB) + "".join(" dh%d 512" % i for i in HALF),
 }
 for _d in _SPEC:
     _w = _SPEC[_d].split()
@@ -71,9 +73,19 @@ def rank_program(g, core, T, topo):
     def D(q, deps, sem, out, in_):
         wait(q, deps); queues[q].dma_start(out, in_).then_inc(T.sem[sem], 16); return tick(sem, 16)
 
+    alt = [False]
+
+    def C(deps, out, in_):
+        return V(deps, v.tensor_copy, out, in_) if alt[0] else S(deps, out, in_, ACT.Copy)
+
+    def A(deps, out, in_, scale, bias):
+        if alt[0]:
+            return V(deps, v.tensor_scalar, out, in_, scale, bias, ALU.mult, ALU.add)
+        return S(deps, out, in_, ACT.Identity, bias=bias, scale=scale)
+
     for q in range(2):
         sn = D("ys"[q], [], "lsn", T.sn8[16 * q:16 * q + 16, :], T.sn[:])
-    u0 = D("y", [], "lu0", T.ua[:, 4 * UC:4 * UC + 16], T.u[:, 0:16])
+    u0 = D("y", [], "lu0", T.ua[:, 4 * UC:4 * UC + 8], T.u[:, 0:8])
     kl = []
     for h in range(2):
         a, b = 512 * h, 512 * h + 512
@@ -100,8 +112,9 @@ def rank_program(g, core, T, topo):
 
     for a in range(1, 4):
         s8 = V([sn], v.tensor_copy, T.sn8[32 * a:32 * a + 32, :], T.sn8[0:32, :])
-    uq = V([u0, z_u], v.quantize_mx, T.uq[:], T.us[:], T.ua[:])
+    u1 = V([u0], v.tensor_copy, T.ua[:, 4 * UC + 8:4 * UC + 16], T.ua[:, 4 * UC:4 * UC + 8])
     lf = V([s8], v.tensor_scalar, T.lf[:], T.sn8[:], 1.0, 1.0, ALU.add, ALU.min)
+    uq = V([u1, z_u], v.quantize_mx, T.uq[:], T.us[:], T.ua[:])
     ur = V([uq, z_l], v.tensor_copy, T.urq[:].bitcast(u32), T.uq[:].bitcast(u32).indirect(T.ul[:]))
     us = S([uq, z_l], T.urs[:], T.us[:].indirect(T.ul[:]), ACT.Copy)
     others = [d for d in range(NR) if d != me]
@@ -126,30 +139,38 @@ def rank_program(g, core, T, topo):
         vo = V([c_vo], v.tensor_copy, T.vo[32 * a:32 * a + 32, :], T.vo0[0:32, :])
     z_m = V([z_e], v.memset, T.ee[0:1, 0:MX], -1.0)
 
-    rv, rs, pc = [], [], []
-    for h in range(2):
+    rv, rs, pc = {}, {}, {}
+
+    def p_cols(k):
+        for i, b in enumerate(CG[k]):
+            c, o = 128 * b, UC - 4 * i
+            pc[k] = P([uq, kl[b // 4]], T.py[:, 512 * k:512 * k + 128], T.winq[:, c:c + 128], T.wins[:, c:c + 128],
+                      T.uq[:, o:o + 128], T.us[:, o:o + 128], i == 0, b == CG[k][-1])
+
+    def p_rows(ps, r, h):
         a, b = 512 * h, 512 * h + 512
-        for i in range(4):
-            c, o = a + 128 * i, UC - 2 * i
-            t = P([uq, kl[h]], T.py[:, a:a + 128], T.winq[:, c:c + 128], T.wins[:, c:c + 128], T.uq[:, o:o + 128], T.us[:, o:o + 128], i == 0, i == 3)
-        pc.append(t)
-        for ps, r in ((T.psv, rv), (T.pss, rs))[::2 * h - 1]:
-            r.append(P([ur, us], ps[:, a:b], T.urq[:], T.urs[:], T.winq[:, a:b], T.wins[:, a:b], True, True))
+        r[h] = P([ur, us, kl[h]], ps[:, a:b], T.urq[:], T.urs[:], T.winq[:, a:b], T.wins[:, a:b], True, True)
+
+    p_cols(0); p_rows(T.pss, rs, 0); p_cols(1); p_rows(T.psv, rv, 0)
+    p_cols(2); p_rows(T.psv, rv, 1); p_rows(T.pss, rs, 1)
 
     R = {}
     w0, own0, m2 = NC + CAP * me, CAP * me, T.incl[:, NR * CAP - 1:NR * CAP]
 
     def own_score(i):
-        return T.xx[:, 32 * i + 1:32 * i + 2]
+        return T.xx[:, i, 1:2]
+
+    def col_of(i):
+        return [R["col%d" % k] for k in range(3) if i in CG[k]]
 
     def runs(h, cut):
-        a, b = 512 * h, 512 * h + 512
+        a, b = ((0, 512), (512, NC), (0, NC))[h]
         m = min(max(cut, a), b)
         return [(lo, hi, k) for k, (lo, hi) in enumerate(((a, m), (m, b))) if lo < hi]
 
     def vrun(i):
-        j = i
-        while j < 8 and j not in SB:
+        j = i + 1
+        while j % 4 and j not in SB:
             j += 1
         return range(i, j)
 
@@ -160,12 +181,14 @@ def rank_program(g, core, T, topo):
         a, b = LISTS[k]
         return T.scn[:, 512 * a + 511:512 * b:512], [R["join%d" % i if i in SB else "sum%d" % i] for i in range(a, b)]
 
-    def col(h):
-        return V([pc[h], z_x], v.tensor_copy, T.xx[:, 128 * h + 1:128 * h + 128:32], T.py[:, 512 * h:512 * h + 8:2])
+    def col(k):
+        c = CG[k]
+        o, p = T.xx[:, c[0]:c[-1] + 1:c[1] - c[0], 1:32:16], T.py[:, 512 * k:512 * k + 4 * len(c):2]
+        return C([pc[k], z_x], o, p)
 
     def dif(i, h):
         for lo, hi, k in runs(h, 128 * i + 128 * (i % 4 == 3)):
-            t = S([rs[h], R["col%d" % (i // 4)]], T["df%d" % i][:, lo + 128 * k:hi + 128 * k], T.pss[:, lo:hi], ACT.Identity, bias=own_score(i), scale=-1.0)
+            t = S([rs[min(h, 1)]] + col_of(i), T["df%d" % i][:, lo + 128 * k:hi + 128 * k], T.pss[:, lo:hi], ACT.Identity, bias=own_score(i), scale=-1.0)
         return t
 
     def msk(i):
@@ -192,14 +215,25 @@ def rank_program(g, core, T, topo):
         return V([R["sgn%da" % i], R["sgn%db" % i]], v.tensor_scalar, T.scn[:, o:o + 1], T.acc1[:, i:i + 1], T.acc2[:, i:i + 1], 0.5, ALU.add, ALU.mult)
 
     def cmp(i, h):
+        n = 512 if i in HALF else NC
         for lo, hi, k in runs(h, 128 * i + 128):
-            t = V([rv[h], R["col%d" % (i // 4)]], v.tensor_scalar, T["cm%d" % i][:, lo:hi], T.psv[:, lo:hi], own_score(i), HW / NC - 1.0,
-                  (ALU.is_gt, ALU.is_ge)[k], ALU.add)
+            t = V([rv[min(h, 1)]] + col_of(i), v.tensor_scalar, T["cm%d" % i][:, lo:hi], T.psv[:, lo:hi], own_score(i),
+                  (HW - (NC - n) // 2) / n - 1.0, (ALU.is_gt, ALU.is_ge)[k], ALU.add)
         return t
+
+    def hd(i):
+        h = 1 - i // 4
+        return S([rs[h]] + col_of(i), T["dh%d" % i][:], T.pss[:, 512 * h:512 * h + 512], ACT.Identity, bias=own_score(i), scale=-1.0)
+
+    def hs(i):
+        return S([R["hd%d" % i]], T["sh%d" % i][:], T["dh%d" % i][:], ACT.Sign, bias=TINY if i < 4 else -TINY, scale=-1.0, accum_out=T.acc1[:, i:i + 1])
+
+    def hj(i):
+        return A([R["hs%d" % i]] + tie_of(i), T.acc2[:, i:i + 1], T.acc1[:, i:i + 1], 0.5, T.eqs[:, 128 * i + 127:128 * i + 128])
 
     def eq(i):
         b = 128 * i
-        return V([R["col%d" % (i // 4)], rv[i // 4]], v.tensor_scalar, T.eq[:, b:b + 128], T.psv[:, b:b + 128], own_score(i), None, ALU.is_equal)
+        return V([rv[i // 4]] + col_of(i), v.tensor_scalar, T.eq[:, b:b + 128], T.psv[:, b:b + 128], own_score(i), None, ALU.is_equal)
 
     def tie(i):
         a, b = 128 * i, 128 * vrun(i)[-1] + 128
@@ -207,6 +241,10 @@ def rank_program(g, core, T, topo):
 
     def vsum(i):
         cm, o, e = T["cm%d" % i], 512 * i, 128 * i + 127
+        if i in HALF:
+            a = 512 * (i // 4)
+            return V([R["cmp%d%s" % (i, "ab"[i // 4])], R["hj%d" % i]], v.tensor_tensor_scan, T.scn[:, o + 256:o + 512], cm[:, a:a + 256],
+                     cm[:, a + 256:a + 512], T.acc2[:, i:i + 1], ALU.add, ALU.add)
         return V([R["cmp%da" % i], R["cmp%db" % i]] + tie_of(i), v.tensor_tensor_scan, T.scn[:, o:o + 512], cm[:, 0:512], cm[:, 512:NC],
                  T.eqs[:, e:e + 1], ALU.add, ALU.add)
 
@@ -221,14 +259,12 @@ def rank_program(g, core, T, topo):
         t = fl0
         for a, b in ((0, LC * me), (LC * me + LC, LC * NR)):
             if a < b:
-                t = S([larr], T.fl[:, 16 * a:16 * b], T.w01[:].indirect(T.lu[:, a:b]), ACT.Copy)
+                t = C([larr, fl0], T.fl[:, 16 * a:16 * b], T.w01[:].indirect(T.lu[:, a:b]))
         return t
 
-    def kb():
-        t = S([R["incl"], c_k], T.kb[:], T.kn[:], ACT.Identity, bias=m2)
-        S([], T.ma[:, 0:1], m2, ACT.Identity, bias=-float(HW), scale=0.5)
-        R["ma"] = S([], T.ma[:, 1:2], m2, ACT.Identity, bias=float(HW), scale=-0.5)
-        return t
+    def ma():
+        A([R["incl"]], T.ma[:, 0:1], m2, 0.5, -float(HW))
+        return A([], T.ma[:, 1:2], m2, -0.5, float(HW))
 
     def cs():
         for h in range(2):
@@ -242,8 +278,8 @@ def rank_program(g, core, T, topo):
 
     def num():
         R["js"] = G([], g.iota, T.js[:], [[128, 8], [0, 2], [1, 16]], 0, 1, **FL)
-        G([z_x], g.iota, T.xx[:, 0:256:16], [[128, 8], [0, 2]], 1, 1, **FL)
-        return G([], g.iota, T.xx[0:16, 0:256:16], [[128, 8], [0, 2]], 0, 1, **FL)
+        G([z_x], g.iota, T.xx[:, :, 0:32:16], [[128, 8], [0, 2]], 1, 1, **FL)
+        return G([], g.iota, T.xx[0:16, :, 0:32:16], [[128, 8], [0, 2]], 0, 1, **FL)
 
     def rk(k):
         (a, b), (cnt, d) = LISTS[k], count(k)
@@ -282,66 +318,74 @@ def rank_program(g, core, T, topo):
 
     def ev(k):
         a, b = LISTS[k]
-        return V([R["rn%d" % k], z_m, R["dd"]] + ([R["ev0"]] if k else []), v.tensor_copy, T.ee[:].indirect(T.rkn[:, 8 * k:8 * k + b - a]), T.dd[:, 16 * a:16 * b])
+        return V([R["rn%d" % k], z_m, R["dd"]] + ([R["ev%d" % (k - 1)]] if k else []), v.tensor_copy, T.ee[:].indirect(T.rkn[:, 8 * k:8 * k + b - a]), T.dd[:, 16 * a:16 * b])
 
     def have(i):
-        return [R["c3%d" % (i // 2)], R["own"], R["snd"]] + kl
+        return [R["c3%d" % sum(PIECES[i][0] >= 128 * b for a, b in LISTS)], R["own"], R["snd"]] + kl
 
     def pv(i):
         a, b = PIECES[i]
-        t = V(have(i), v.tensor_copy, T.aftq[:, a:b].bitcast(u32), T.winq[:].bitcast(u32).indirect(T.off[:, a // 16:b // 16]))
-        D("y", [t], "sto", T.oc[:, 4 * a:4 * b], T.aftq[:, a:b].bitcast(u8))
-        return t
+        return V(have(i), v.tensor_copy, T.aftq[:, a:b].bitcast(u32), T.winq[:].bitcast(u32).indirect(T.off[:, a // 16:b // 16]))
+
+    def oc(i):
+        a, b = PIECES[i]
+        return D("ys"[alt[0]], [R["pv%d" % i]], "sto", T.oc[:, 4 * a:4 * b], T.aftq[:, a:b].bitcast(u8))
+
+    def ys(i):
+        a, b = PIECES[i]
+        return D("ys"[alt[0]], [R["y%d" % i]], "sto", T.y[:, a:b], T.ysb[:, a:b])
 
     def psc(i):
         a, b = PIECES[i]
-        return S(have(i), T.afts[:, a:b], T.wins[:].indirect(T.off[:, a // 16:b // 16]), ACT.Copy)
+        return C(have(i), T.afts[:, a:b], T.wins[:].indirect(T.off[:, a // 16:b // 16]))
 
     def mm(i):
-        a, b = PIECES[i]
-        return P([R["pv%d" % i], R["ps%d" % i], R["wq"], R["col0"], R["col1"]], T.py[:, 512 * i:512 * i + b - a], T.wq[:], T.wsc[:],
-                 T.aftq[:, a:b], T.afts[:, a:b], True, True)
+        (a, b), o = PIECES[i], 512 * (i % 4)
+        return P([R["pv%d" % i], R["ps%d" % i], R["wq"], R["col0"], R["col1"], R["col2"]] + ([R["y%d" % (i - 4)]] if i > 3 else []),
+                 T.py[:, o:o + b - a], T.wq[:], T.wsc[:], T.aftq[:, a:b], T.afts[:, a:b], True, True)
 
     def y(i):
-        a, b = PIECES[i]
-        t = S([R["mm%d" % i]], T.ysb[:, a:b], T.py[:, 512 * i:512 * i + b - a], ACT.Copy)
-        return D("y", [t], "sto", T.y[:, a:b], T.ysb[:, a:b])
+        (a, b), o = PIECES[i], 512 * (i % 4)
+        return C([R["mm%d" % i]], T.ysb[:, a:b], T.py[:, o:o + b - a])
 
-    def osc():
-        for k in range(4):
-            D("y", [R["ps%d" % i] for i in range(4)], "sto", T.osc[4 * k:4 * k + 4, :], T.afts[32 * k:32 * k + 4, :])
+    def os(k):
+        return D("ys"[alt[0]], [R["ps%d" % i] for i in range(len(PIECES))], "sto", T.osc[4 * k:4 * k + 4, :], T.afts[32 * k:32 * k + 4, :])
 
-    def l1():
-        for e in range(2):
-            t = V([R["et"]], v.tensor_tensor, T.l1[:, 8 * e:8 * e + 8], T.et[:, :, e], T.et[:, :, 16 + e], ALU.add)
-        return t
+    def eo(e):
+        return D("ys"[alt[0]], [R["l4"]], "sto", T.ev[e:e + 1, :], T.l4[e:16:2, :])
 
     plain = {
         "xq": lambda: V([xl], v.quantize_mx, T.xq[:], T.xs[:], T.xt[:]),
         "pq": lambda: V([R["xq"], su], v.tensor_copy, T.sndq[:].bitcast(u32), T.xq[:].bitcast(u32).indirect(T.su[:])),
-        "ps": lambda: S([R["xq"], su], T.snds[:], T.xs[:].indirect(T.su[:]), ACT.Copy),
+        "ps": lambda: C([R["xq"], su], T.snds[:], T.xs[:].indirect(T.su[:])),
         "wq": lambda: V([wl], v.quantize_mx, T.wq[:], T.wsc[:], T.wt[:]),
         "incl": lambda: V([R["fl"]], v.tensor_tensor_scan, T.incl[:], T.fl[:], T.fl[:], 0.0, ALU.add, ALU.max),
-        "sl": lambda: S([R["cs"], z_a], T.a2[:, 0:64:32], T.csum[:], ACT.Identity, bias=float(NC + NR * CAP // 2), scale=0.5),
+        "kb": lambda: A([R["incl"], c_k], T.kb[:], T.kn[:], 1.0, m2),
+        "sl": lambda: A([R["cs"], z_a], T.a2[:, 0:64:32], T.csum[:], 0.5, float(NC + NR * CAP // 2)),
         "b2": lambda: V([R["sl"]], v.transpose, T.b2[:], T.a2[:]),
-        "x2": lambda: S([R["col0"], R["col1"]], T.xx[:, 17:256:32], T.xx[:, 1:256:32], ACT.Copy),
-        "xr": lambda: V([R["x2"], R["num"]], v.transpose, T.xr[:], T.xx[:]),
-        "dd": lambda: S([R["xr"], vo], T.dd[:], T.xr[:].indirect(T.vo[:]), ACT.Copy),
-        "et": lambda: V([R["ev1"]], v.transpose, T.et[:], T.ee[:, 0:MX]),
+        "xr": lambda: V([R["col0"], R["col1"], R["col2"], R["num"]], v.transpose, T.xr[:], T.xx[:]),
+        "dd": lambda: C([R["xr"], vo], T.dd[:], T.xr[:].indirect(T.vo[:])),
+        "et": lambda: V([R["ev%d" % (len(LISTS) - 1)]], v.transpose, T.et[:], T.ee[:, 0:MX]),
+        "l1": lambda: V([R["et"]], v.tensor_tensor, T.l1[:], T.et[:, :, 0:2], T.et[:, :, 16:18], ALU.add),
         "l2": lambda: V([R["l1"]], v.tensor_tensor, T.l2[0:64, :], T.l1[0:64, :], T.l1[64:128, :], ALU.add),
         "l3": lambda: V([R["l2"], z_3], v.tensor_tensor, T.l3[0:32, 0:16], T.l2[0:32, :], T.l2[32:64, :], ALU.add),
         "l4": lambda: V([R["l3"]], v.transpose, T.l4[0:32, :], T.l3[0:32, :]),
-        "evo": lambda: D("s", [R["l4"]], "sto", T.ev[:], T.l4[0:16, :]),
-        "snd": snd, "fl": fl, "kb": kb, "cs": cs, "pb": pb, "num": num, "osc": osc, "l1": l1,
+        "dv": lambda: V([rv[1]], v.tensor_copy, T.dum[:], T.psv[:]),
+        "ds": lambda: S([rs[1]], T.dum[:], T.pss[:], ACT.Copy),
+        "snd": snd, "fl": fl, "ma": ma, "cs": cs, "pb": pb, "num": num,
     }
     numbered = {"col": col, "msk": msk, "join": join, "eq": eq, "tie": tie, "sum": vsum, "rk": rk, "pt": pt, "tr": tr, "c3": c3,
-                "gg": gg, "uu": uu, "rn": rn, "ev": ev, "pv": pv, "ps": psc, "mm": mm, "y": y}
+                "gg": gg, "uu": uu, "rn": rn, "ev": ev, "pv": pv, "ps": psc, "mm": mm, "y": y, "oc": oc, "ys": ys, "os": os, "eo": eo, "hd": hd, "hs": hs, "hj": hj}
     halved = {"dif": dif, "sgn": sgn, "cmp": cmp}
     for name in ORDER.split():
+        alt[0] = name.endswith("!")
+        name = name.rstrip("!")
         if name in plain:
             R[name] = plain[name]()
         elif name[-1] in "ab":
             R[name] = halved[name[:-2]](int(name[-2]), "ab".index(name[-1]))
+        elif name[-1] == "w":
+            R[name[:-1] + "a"] = R[name[:-1] + "b"] = halved[name[:-2]](int(name[-2]), 2)
         else:
             R[name] = numbered[name[:-1]](int(name[-1]))
 

@@ -1,43 +1,49 @@
 from concourse.bass import DstId, RemoteDMATransfer
 from concourse.mybir import dt, AluOpType as ALU, ActivationFunctionType as ACT
 
-NR, NT, NC, CAP, MX = 4, 512, 1024, 96, 256
-NW = NC + NR * CAP
+NR, NC, CAP, MX = 4, 1024, 96, 256
 LC = CAP // 16
 WD = NC + 128
 HW = WD // 2
+MID = NC + NR * CAP // 2
 TINY = 2.0 ** -120
 UC = 12
 SB = (0, 3, 7)
-HALF = (6,)
+HALF = {6: 512}
+TIES = ((1, 2), (4, 5, 6))
 CG = ((0, 3), (1, 2), (4, 5, 6, 7))
-LISTS = ((0, 5), (5, 8))
-PIECES = ((0, 320), (320, 640), (640, 896), (896, 1024))
+PEO = "c0 s0 c1 v0 c2 v1 s1"
+LOADS = "y:sn0 s:sn1 y:u y:kc0 y:ks0 y:x y:kc1 y:ks1 y:w"
+LISTS = ((0, 6), (6, 8))
+PIECES = ((0, 384), (384, 768), (768, 896), (896, 1024))
+OCS = ((0,), (1,), (2, 3))
+YSS = ((0,), (1,), (2, 3))
 ORDER = """
-col0! col1 dif3a xq dif0a cmp1a ps msk3 cmp2a eq1 eq2 msk0 sgn3a pq col2 tie1 cmp2b snd fl eq6 cmp1b num sgn0a dif3b incl sum2 dif7w
-kb! cmp4w cs msk7 cmp5w dif0b sl! sgn3b eq4 b2 eq5 pb cmp6b sgn0b join3 tie4 sum1 sum4 ma hd6 xr join0 wq sgn7b rk0 hs6 sum5 pt0 hj6
-gg0 sgn7a tr0 sum6 c30 uu0 pv0 ps0 join7 dd pv1 oc0 mm0 ps1 rk1 oc1 rn0 y0 gg1 mm1 pt1 uu1 ys0 y1 tr1 rn1 ys1 c31 ev0 ps3 ps2 pv3 pv2
-mm3 oc3 os3! os1 y3 ev1 os2! mm2 oc2 ys3 et y2 os0! l1 ys2 l2 l3 l4 eo0! eo1
+col0! dif3a xq dif0a msk3 col1! pq ps snd cmp1a eq1 msk0 sgn3a eq2 col2! cmp2a hd6 tv0 eq5 fl num cmp5w sgn0a dif7w incl eq4 kb! eq6 cs
+msk7 cmp2b cmp4w dif0b dif3b b2 cmp1b pb sgn0b tv1 sum1 sum5 sgn3b sum4 cmp6b hs6 join0 sum2 ma join3 xr sgn7a
+rk0 wq pt0 hj6! tr0 sgn7b sum6 c30 join7 pv0 ps0 rk1 ps1 oc0 mm0 pv1 dd gg0 pt1 mm1 oc1 y0 uu0 tr1 rn0 ys0 y1 c31 ev0
+ps2 ys1 ps3 pv2 os0! os1 pv3 mm2 et mm3 oc2 y2 y3 os3 l1 l2 os2! ys2 l3 l4 eo1! eo0
 """
 
 SCRATCH = {"psv": ("psum", [128, 1024], "float32"), "pss": ("psum", [128, 1024], "float32"), "py": ("psum", [128, 2048], "float32"),
-           "tt": ("sbuf", [128, 32, 32], "float16"), "et": ("sbuf", [128, 8, 32], "float32"), "xx": ("sbuf", [128, 8, 32], "float32")}
+           "tt": ("sbuf", [128, 32, 32], "float16"), "et": ("sbuf", [128, 8, 32], "float32"), "xx": ("sbuf", [128, 8, 32], "float32"),
+           "cm": ("sbuf", [128, 8, 1024], "bfloat16")}
 _SPEC = {
     "float8_e4m3fn_x4": "uq 142 urq 128 xq 512 wq 128 sndq 384 winq 1408 aftq 1024",
     "uint8": "us 142 urs 128 xs 512 wsc 128 snds 384 wins 1408 afts 1024",
     "int32": "sn8 24 vo0 8",
-    "uint16": "su 24 lf 24 lu 24 ul 8 rkd 16 rkn 24 off 64 vo 8",
+    "uint16": "su 24 lf 24 lu 24 ul 8 rkd 16 rkn 8 off 64 vo 8",
     "bfloat16": "ua 568 xt 2048 wt 512 eq 1024 eqs 1024 tri 384 w01 16 fl 384 incl 384 csg 768 "
-                + " ".join("sg%d 1152" % i if i in SB else "cm%d 1024" % i for i in range(8)) + "".join(" sh%d 512" % i for i in HALF),
+                + " ".join("sg%d 1152" % i for i in SB) + "".join(" sh%d %d" % x for x in HALF.items()),
     "float16": "scn 4096 pt 256",
-    "float32": "acc1 8 acc2 8 csum 2 a2 64 b2 64 tb 264 ysb 1024 kn 2 kb 2 ma 2 js 256 dum 1024 xr 256 dd 128 "
-               "ee 1280 gg 8 uu 8 l1 16 l2 16 l3 32 l4 32 " + " ".join("df%d 1152" % i for i in SB) + "".join(" dh%d 512" % i for i in HALF),
+    "float32": "acc1 8 acc2 8 a2 64 b2 64 tb 264 ysb 1024 kn 3 kb 3 tj 128 ma 1 js 256 m1 1 xr 256 dd 128 ee 1280 gg 8 uu 8 "
+               "l1 16 l2 16 l3 32 l4 32 " + " ".join("df%d 1152" % i for i in SB) + "".join(" dh%d %d" % x for x in HALF.items()),
 }
 for _d in _SPEC:
     _w = _SPEC[_d].split()
     for _i in range(0, len(_w), 2):
         SCRATCH[_w[_i]] = ("sbuf", [128, int(_w[_i + 1])], _d)
-SEMAPHORES = "qv qs qt qg lsn lu0 lk0 lk1 lx lw own sto larr carr sent".split()
+SEMAPHORES = "qv qs qt qg lsn lu0 lk0 lk1 lx lw ltb own sto larr carr sent".split()
 
 
 def rank_program(g, core, T, topo):
@@ -83,38 +89,39 @@ def rank_program(g, core, T, topo):
             return V(deps, v.tensor_scalar, out, in_, scale, bias, ALU.mult, ALU.add)
         return S(deps, out, in_, ACT.Identity, bias=bias, scale=scale)
 
-    for q in range(2):
-        sn = D("ys"[q], [], "lsn", T.sn8[16 * q:16 * q + 16, :], T.sn[:])
-    u0 = D("y", [], "lu0", T.ua[:, 4 * UC:4 * UC + 8], T.u[:, 0:8])
-    kl = []
+    what = {"u": ("lu0", T.ua[:, 4 * UC:4 * UC + 8], T.u[:, 0:8]), "x": ("lx", T.xt[:], T.x[:]), "w": ("lw", T.wt[:], T.w[:])}
     for h in range(2):
         a, b = 512 * h, 512 * h + 512
-        D("y", [], "lk%d" % h, T.winq[:, a:b].bitcast(u8), T.kc[:, 4 * a:4 * b])
-        kl.append(D("y", [], "lk%d" % h, T.wins[:, a:b], T.ks[:, a:b]))
-        if h == 0:
-            xl = D("y", [], "lx", T.xt[:], T.x[:])
-    wl = D("y", [], "lw", T.wt[:], T.w[:])
+        what["sn%d" % h] = ("lsn", T.sn8[16 * h:16 * h + 16, :], T.sn[:])
+        what["kc%d" % h] = ("lk%d" % h, T.winq[:, a:b].bitcast(u8), T.kc[:, 4 * a:4 * b])
+        what["ks%d" % h] = ("lk%d" % h, T.wins[:, a:b], T.ks[:, a:b])
+    for x in LOADS.split():
+        D(x[0], [], *what[x[2:]])
+    sn, u0, xl, wl, kl = ("lsn", 32), ("lu0", 16), ("lx", 16), ("lw", 16), [("lk0", 32), ("lk1", 32)]
 
     V([], v.memset, T.ua[:, 0:4 * UC], 0.0)
     z_u = V([], v.memset, T.ua[:, 4 * UC + 16:], 0.0)
     z_l = V([], v.memset, T.ul[:], UC)
     V([], v.memset, T.w01[:, 0:1], 0.0)
-    z_w = V([], v.memset, T.w01[:, 1:16], 2.0)
+    z_w = V([], v.memset, T.w01[:, 1:16], 1.0)
     zero = T.ua[:, 64:320]
-    z_x = S([z_u], T.xx[:], zero, ACT.Copy)
-    z_e = S([], T.ee[:, 0:MX], zero, ACT.Copy)
-    z_a = S([], T.a2[:], T.ua[:, 64:128], ACT.Copy)
-    z_t = S([], T.tb[:, 0:1], T.ua[:, 64:65], ACT.Copy)
-    z_3 = S([], T.l3[0:32, :], T.ua[0:32, 64:96], ACT.Copy)
-    for a in range(4):
-        c_k = G([], g.iota, T.kn[32 * a:32 * a + 32, :], [[-64, 2]], -1 - 128 * a, -2, **FL)
     c_vo = G([], g.iota, T.vo0[:], [[32, 8]], 0, 1)
+    c_j = G([], g.iota, T.tj[:], [[1, 128]], 0, -1, **FL)
+    t = V([c_vo], v.tensor_scalar, T.m1[:], T.vo0[:, 0:1], 0.5, -1.0, ALU.is_lt, ALU.mult)
+    z_x = S([z_u], T.xx[:], zero, ACT.Copy)
+    z_a = S([], T.a2[:], T.ua[:, 64:128], ACT.Copy)
+    z_t = S([], T.tb[:], T.ua[:, 64:328], ACT.Identity, bias=-4096.0)
+    z_3 = S([], T.l3[0:32, :], T.ua[0:32, 64:96], ACT.Copy)
+    z_m = S([t], T.ee[:, 0:MX], zero, ACT.Identity, bias=T.m1[:])
+    for a in range(4):
+        vo = V([], v.tensor_copy, T.vo[32 * a:32 * a + 32, :], T.vo0[0:32, :])
 
-    for a in range(1, 4):
-        s8 = V([sn], v.tensor_copy, T.sn8[32 * a:32 * a + 32, :], T.sn8[0:32, :])
+    for a in range(4):
+        lf = V([sn], v.tensor_scalar, T.lf[32 * a:32 * a + 32, :], T.sn8[0:32, :], 1.0, 1.0, ALU.add, ALU.min)
     u1 = V([u0], v.tensor_copy, T.ua[:, 4 * UC + 8:4 * UC + 16], T.ua[:, 4 * UC:4 * UC + 8])
-    lf = V([s8], v.tensor_scalar, T.lf[:], T.sn8[:], 1.0, 1.0, ALU.add, ALU.min)
+    V([], v.tensor_copy, T.su[0:32, :], T.sn8[0:32, :])
     uq = V([u1, z_u], v.quantize_mx, T.uq[:], T.us[:], T.ua[:])
+    V([], v.tensor_copy, T.su[32:64, :], T.sn8[0:32, :])
     ur = V([uq, z_l], v.tensor_copy, T.urq[:].bitcast(u32), T.uq[:].bitcast(u32).indirect(T.ul[:]))
     us = S([uq, z_l], T.urs[:], T.us[:].indirect(T.ul[:]), ACT.Copy)
     others = [d for d in range(NR) if d != me]
@@ -133,11 +140,15 @@ def rank_program(g, core, T, topo):
     send([lf], "larr", lambda d: T.lf[:, LC * d:LC * d + LC], lambda d: T.lu[:, LC * me:LC * me + LC])
     larr = tick("larr", 2 * len(others))
     fl0 = S([lf, z_w], T.fl[:, CAP * me:CAP * me + CAP], T.w01[:].indirect(T.lf[:, LC * me:LC * me + LC]), ACT.Copy)
-    c_t = G([z_u], g.affine_select, T.tri[:], T.ua[:, 64:448], [[0, 3], [-1, 128]], ALU.is_ge, 1.0, 0, 1)
-    su = V([], v.tensor_copy, T.su[:], T.sn8[:])
+    for a in range(2, 4):
+        su = V([], v.tensor_copy, T.su[32 * a:32 * a + 32, :], T.sn8[0:32, :])
+    t = V([c_j], v.tensor_scalar, T.tri[:, 0:128], T.tj[:], 0.0, None, ALU.is_gt)
+    for a in range(1, 3):
+        c_t = S([t], T.tri[:, 128 * a:128 * a + 128], T.tri[:, 0:128], ACT.Copy)
     for a in range(4):
-        vo = V([c_vo], v.tensor_copy, T.vo[32 * a:32 * a + 32, :], T.vo0[0:32, :])
-    z_m = V([z_e], v.memset, T.ee[0:1, 0:MX], -1.0)
+        V([], v.tensor_scalar, T.kn[32 * a:32 * a + 32, 0:2], T.vo0[0:32, 0:2], -1.0, -0.5 - 64 * a, ALU.mult, ALU.add)
+    c_k = V([], v.memset, T.kn[:, 2:3], -float(HW))
+    c_js = G([], g.iota, T.js[:], [[256, 8], [0, 2], [2, 16]], -2 * MID, 2, **FL)
 
     rv, rs, pc = {}, {}, {}
 
@@ -151,11 +162,14 @@ def rank_program(g, core, T, topo):
         a, b = 512 * h, 512 * h + 512
         r[h] = P([ur, us, kl[h]], ps[:, a:b], T.urq[:], T.urs[:], T.winq[:, a:b], T.wins[:, a:b], True, True)
 
-    p_cols(0); p_rows(T.pss, rs, 0); p_cols(1); p_rows(T.psv, rv, 0)
-    p_cols(2); p_rows(T.psv, rv, 1); p_rows(T.pss, rs, 1)
+    for x in PEO.split():
+        if x[0] == "c":
+            p_cols(int(x[1]))
+        else:
+            p_rows(*{"v": (T.psv, rv), "s": (T.pss, rs)}[x[0]], int(x[1]))
 
     R = {}
-    w0, own0, m2 = NC + CAP * me, CAP * me, T.incl[:, NR * CAP - 1:NR * CAP]
+    w0, own0, m = NC + CAP * me, CAP * me, T.incl[:, NR * CAP - 1:NR * CAP]
 
     def own_score(i):
         return T.xx[:, i, 1:2]
@@ -163,28 +177,21 @@ def rank_program(g, core, T, topo):
     def col_of(i):
         return [R["col%d" % k] for k in range(3) if i in CG[k]]
 
-    def runs(h, cut):
-        a, b = ((0, 512), (512, NC), (0, NC))[h]
-        m = min(max(cut, a), b)
-        return [(lo, hi, k) for k, (lo, hi) in enumerate(((a, m), (m, b))) if lo < hi]
-
-    def vrun(i):
-        j = i + 1
-        while j % 4 and j not in SB:
-            j += 1
-        return range(i, j)
-
     def tie_of(i):
-        return [R["tie%d" % k] for k in range(8) if "tie%d" % k in R and i in vrun(k)]
+        return [R["tv%d" % k] for k in range(len(TIES)) if i in TIES[k]]
 
-    def count(k):
-        a, b = LISTS[k]
+    def runs(h, cut, first=0):
+        a, b = ((0, 512), (512, NC), (0, NC))[h]
+        a = max(a, first)
+        c = min(max(cut, a), b)
+        return [(lo, hi, k) for k, (lo, hi) in enumerate(((a, c), (c, b))) if lo < hi]
+
+    def count(a, b):
         return T.scn[:, 512 * a + 511:512 * b:512], [R["join%d" % i if i in SB else "sum%d" % i] for i in range(a, b)]
 
     def col(k):
         c = CG[k]
-        o, p = T.xx[:, c[0]:c[-1] + 1:c[1] - c[0], 1:32:16], T.py[:, 512 * k:512 * k + 4 * len(c):2]
-        return C([pc[k], z_x], o, p)
+        return C([pc[k], z_x], T.xx[:, c[0]:c[-1] + 1:c[1] - c[0], 1:32:16], T.py[:, 512 * k:512 * k + 4 * len(c):2])
 
     def dif(i, h):
         for lo, hi, k in runs(h, 128 * i + 128 * (i % 4 == 3)):
@@ -215,38 +222,34 @@ def rank_program(g, core, T, topo):
         return V([R["sgn%da" % i], R["sgn%db" % i]], v.tensor_scalar, T.scn[:, o:o + 1], T.acc1[:, i:i + 1], T.acc2[:, i:i + 1], 0.5, ALU.add, ALU.mult)
 
     def cmp(i, h):
-        n = 512 if i in HALF else NC
-        for lo, hi, k in runs(h, 128 * i + 128):
-            t = V([rv[min(h, 1)]] + col_of(i), v.tensor_scalar, T["cm%d" % i][:, lo:hi], T.psv[:, lo:hi], own_score(i),
-                  (HW - (NC - n) // 2) / n - 1.0, (ALU.is_gt, ALU.is_ge)[k], ALU.add)
+        f = HALF.get(i, 0)
+        for lo, hi, k in runs(h, 128 * i + 128, f):
+            t = V([rv[min(h, 1)]] + col_of(i), v.tensor_scalar, T.cm[:, i, lo:hi], T.psv[:, lo:hi], own_score(i),
+                  (HW - f // 2) / (NC - f) - 1.0, (ALU.is_gt, ALU.is_ge)[k], ALU.add)
         return t
-
-    def hd(i):
-        h = 1 - i // 4
-        return S([rs[h]] + col_of(i), T["dh%d" % i][:], T.pss[:, 512 * h:512 * h + 512], ACT.Identity, bias=own_score(i), scale=-1.0)
-
-    def hs(i):
-        return S([R["hd%d" % i]], T["sh%d" % i][:], T["dh%d" % i][:], ACT.Sign, bias=TINY if i < 4 else -TINY, scale=-1.0, accum_out=T.acc1[:, i:i + 1])
-
-    def hj(i):
-        return A([R["hs%d" % i]] + tie_of(i), T.acc2[:, i:i + 1], T.acc1[:, i:i + 1], 0.5, T.eqs[:, 128 * i + 127:128 * i + 128])
 
     def eq(i):
         b = 128 * i
         return V([rv[i // 4]] + col_of(i), v.tensor_scalar, T.eq[:, b:b + 128], T.psv[:, b:b + 128], own_score(i), None, ALU.is_equal)
 
-    def tie(i):
-        a, b = 128 * i, 128 * vrun(i)[-1] + 128
-        return V([R["eq%d" % k] for k in vrun(i)] + [c_t], v.tensor_tensor_scan, T.eqs[:, a:b], T.tri[:, 0:b - a], T.eq[:, a:b], 0.0, ALU.mult, ALU.add)
+    def tv(i):
+        a, b = 128 * TIES[i][0], 128 * TIES[i][-1] + 128
+        return V([R["eq%d" % k] for k in TIES[i]] + [c_t], v.tensor_tensor_scan, T.eqs[:, a:b], T.tri[:, 0:b - a], T.eq[:, a:b], 0.0, ALU.mult, ALU.add)
+
+    def hd(i):
+        return S([rs[HALF[i] > 512]] + col_of(i), T["dh%d" % i][:], T.pss[:, 0:HALF[i]], ACT.Identity, bias=own_score(i), scale=-1.0)
+
+    def hs(i):
+        return S([R["hd%d" % i]], T["sh%d" % i][:], T["dh%d" % i][:], ACT.Sign, bias=-TINY, scale=-1.0, accum_out=T.acc1[:, i:i + 1])
+
+    def hj(i):
+        return A([R["hs%d" % i]] + tie_of(i), T.acc2[:, i:i + 1], T.acc1[:, i:i + 1], 0.5, T.eqs[:, 128 * i + 127:128 * i + 128])
 
     def vsum(i):
-        cm, o, e = T["cm%d" % i], 512 * i, 128 * i + 127
-        if i in HALF:
-            a = 512 * (i // 4)
-            return V([R["cmp%d%s" % (i, "ab"[i // 4])], R["hj%d" % i]], v.tensor_tensor_scan, T.scn[:, o + 256:o + 512], cm[:, a:a + 256],
-                     cm[:, a + 256:a + 512], T.acc2[:, i:i + 1], ALU.add, ALU.add)
-        return V([R["cmp%da" % i], R["cmp%db" % i]] + tie_of(i), v.tensor_tensor_scan, T.scn[:, o:o + 512], cm[:, 0:512], cm[:, 512:NC],
-                 T.eqs[:, e:e + 1], ALU.add, ALU.add)
+        a, o = HALF.get(i, 0), 512 * i + 512
+        n = (NC - a) // 2
+        d, first = ([R["hj%d" % i]], T.acc2[:, i:i + 1]) if a else ([R["cmp%da" % i]] + tie_of(i), T.eqs[:, 128 * i + 127:128 * i + 128])
+        return V(d + [R["cmp%db" % i]], v.tensor_tensor_scan, T.scn[:, o - n:o], T.cm[:, i, a:a + n], T.cm[:, i, a + n:NC], first, ALU.add, ALU.add)
 
     def snd():
         send([R["pq"]], "carr", lambda d: T.sndq[:, CAP * d:CAP * d + CAP].bitcast(u8), lambda d: T.winq[:, w0:w0 + CAP].bitcast(u8))
@@ -262,34 +265,30 @@ def rank_program(g, core, T, topo):
                 t = C([larr, fl0], T.fl[:, 16 * a:16 * b], T.w01[:].indirect(T.lu[:, a:b]))
         return t
 
-    def ma():
-        A([R["incl"]], T.ma[:, 0:1], m2, 0.5, -float(HW))
-        return A([], T.ma[:, 1:2], m2, -0.5, float(HW))
-
     def cs():
         for h in range(2):
-            t = S([R["kb"]], T.csg[:, 384 * h:384 * h + 384], T.incl[:], ACT.Sign, bias=T.kb[:, h:h + 1], scale=-1.0, accum_out=T.csum[:, h:h + 1])
+            t = S([R["kb"], z_a], T.csg[:, 384 * h:384 * h + 384], T.incl[:], ACT.Sign, bias=T.kb[:, h:h + 1], scale=-1.0,
+                  accum_out=T.a2[:, 32 * h:32 * h + 1])
         return t
 
     def pb():
-        for a in range(4):
-            t = G([R["b2"]], g.partition_broadcast, T.tb[:, 1 + 64 * a:65 + 64 * a], T.b2[32 * a:32 * a + 1, :], 128)
+        for q in range(8):
+            t = D("y", [R["b2"], z_t], "ltb", T.tb[16 * q:16 * q + 1, 1:MX + 1], T.b2[0:128:32, :])
         return t
 
     def num():
-        R["js"] = G([], g.iota, T.js[:], [[128, 8], [0, 2], [1, 16]], 0, 1, **FL)
         G([z_x], g.iota, T.xx[:, :, 0:32:16], [[128, 8], [0, 2]], 1, 1, **FL)
         return G([], g.iota, T.xx[0:16, :, 0:32:16], [[128, 8], [0, 2]], 0, 1, **FL)
 
     def rk(k):
-        (a, b), (cnt, d) = LISTS[k], count(k)
+        (a, b), (cnt, d) = LISTS[k], count(*LISTS[k])
         for e in range(2):
-            t = V(d + [R["ma"]], v.tensor_scalar, T.rkd[:, 2 * a + e:2 * b:2], cnt, T.ma[:, 0:1], 0.0, ALU.add, ALU.max)
+            t = V(d + [R["kb"]], v.tensor_scalar, T.rkd[:, 2 * a + e:2 * b:2], cnt, T.kb[:, 2:3], 0.0, ALU.add, ALU.max)
         return t
 
     def pt(k):
         a, b = LISTS[k]
-        return V([R["rk%d" % k], R["pb"], z_t, R["js"]], v.tensor_tensor, T.pt[:, 32 * a:32 * b], T.tb[:].indirect(T.rkd[:, 2 * a:2 * b]),
+        return V([R["rk%d" % k], R["pb"], z_t, c_js], v.tensor_tensor, T.pt[:, 32 * a:32 * b], T.tb[:, 0:MX + 1].indirect(T.rkd[:, 2 * a:2 * b]),
                  T.js[:, 32 * a:32 * b], ALU.max)
 
     def tr(k):
@@ -301,24 +300,9 @@ def rank_program(g, core, T, topo):
     def c3(k):
         a, b = LISTS[k]
         for q in range(4):
-            t = V([R["tr%d" % k]], v.tensor_copy, T.off[32 * q:32 * q + 32, 8 * a:8 * b], T.tt[0:32, 4 * a:4 * b, 0:32:16])
+            t = V([R["tr%d" % k]], v.tensor_scalar, T.off[32 * q:32 * q + 32, 8 * a:8 * b], T.tt[0:32, 4 * a:4 * b, 0:32:16], 0.5, float(MID),
+                  ALU.mult, ALU.add)
         return t
-
-    def gg(k):
-        (a, b), (cnt, d) = LISTS[k], count(k)
-        return V(d + [R["ma"]], v.tensor_scalar, T.gg[:, a:b], cnt, T.ma[:, 1:2], float(MX), ALU.is_le, ALU.mult)
-
-    def uu(k):
-        (a, b), (cnt, d) = LISTS[k], count(k)
-        return V([R["gg%d" % k]], v.tensor_tensor, T.uu[:, a:b], T.gg[:, a:b], cnt, ALU.subtract)
-
-    def rn(k):
-        a, b = LISTS[k]
-        return V([R["uu%d" % k]], v.tensor_scalar, T.rkn[:, 8 * k:8 * k + b - a], T.uu[:, a:b], float(HW), None, ALU.add)
-
-    def ev(k):
-        a, b = LISTS[k]
-        return V([R["rn%d" % k], z_m, R["dd"]] + ([R["ev%d" % (k - 1)]] if k else []), v.tensor_copy, T.ee[:].indirect(T.rkn[:, 8 * k:8 * k + b - a]), T.dd[:, 16 * a:16 * b])
 
     def have(i):
         return [R["c3%d" % sum(PIECES[i][0] >= 128 * b for a, b in LISTS)], R["own"], R["snd"]] + kl
@@ -327,28 +311,28 @@ def rank_program(g, core, T, topo):
         a, b = PIECES[i]
         return V(have(i), v.tensor_copy, T.aftq[:, a:b].bitcast(u32), T.winq[:].bitcast(u32).indirect(T.off[:, a // 16:b // 16]))
 
-    def oc(i):
-        a, b = PIECES[i]
-        return D("ys"[alt[0]], [R["pv%d" % i]], "sto", T.oc[:, 4 * a:4 * b], T.aftq[:, a:b].bitcast(u8))
-
-    def ys(i):
-        a, b = PIECES[i]
-        return D("ys"[alt[0]], [R["y%d" % i]], "sto", T.y[:, a:b], T.ysb[:, a:b])
-
     def psc(i):
         a, b = PIECES[i]
         return C(have(i), T.afts[:, a:b], T.wins[:].indirect(T.off[:, a // 16:b // 16]))
 
     def mm(i):
-        (a, b), o = PIECES[i], 512 * (i % 4)
-        return P([R["pv%d" % i], R["ps%d" % i], R["wq"], R["col0"], R["col1"], R["col2"]] + ([R["y%d" % (i - 4)]] if i > 3 else []),
-                 T.py[:, o:o + b - a], T.wq[:], T.wsc[:], T.aftq[:, a:b], T.afts[:, a:b], True, True)
+        a, b = PIECES[i]
+        return P([R["pv%d" % i], R["ps%d" % i], R["wq"], R["col0"], R["col1"], R["col2"]], T.py[:, 512 * i:512 * i + b - a],
+                 T.wq[:], T.wsc[:], T.aftq[:, a:b], T.afts[:, a:b], True, True)
 
     def y(i):
-        (a, b), o = PIECES[i], 512 * (i % 4)
-        return C([R["mm%d" % i]], T.ysb[:, a:b], T.py[:, o:o + b - a])
+        a, b = PIECES[i]
+        return C([R["mm%d" % i]], T.ysb[:, a:b], T.py[:, 512 * i:512 * i + b - a])
 
-    def os(k):
+    def oc(i):
+        a, b = PIECES[OCS[i][0]][0], PIECES[OCS[i][-1]][1]
+        return D("ys"[alt[0]], [R["pv%d" % k] for k in OCS[i]], "sto", T.oc[:, 4 * a:4 * b], T.aftq[:, a:b].bitcast(u8))
+
+    def ys(i):
+        a, b = PIECES[YSS[i][0]][0], PIECES[YSS[i][-1]][1]
+        return D("ys"[alt[0]], [R["y%d" % k] for k in YSS[i]], "sto", T.y[:, a:b], T.ysb[:, a:b])
+
+    def osk(k):
         return D("ys"[alt[0]], [R["ps%d" % i] for i in range(len(PIECES))], "sto", T.osc[4 * k:4 * k + 4, :], T.afts[32 * k:32 * k + 4, :])
 
     def eo(e):
@@ -360,22 +344,24 @@ def rank_program(g, core, T, topo):
         "ps": lambda: C([R["xq"], su], T.snds[:], T.xs[:].indirect(T.su[:])),
         "wq": lambda: V([wl], v.quantize_mx, T.wq[:], T.wsc[:], T.wt[:]),
         "incl": lambda: V([R["fl"]], v.tensor_tensor_scan, T.incl[:], T.fl[:], T.fl[:], 0.0, ALU.add, ALU.max),
-        "kb": lambda: A([R["incl"], c_k], T.kb[:], T.kn[:], 1.0, m2),
-        "sl": lambda: A([R["cs"], z_a], T.a2[:, 0:64:32], T.csum[:], 0.5, float(NC + NR * CAP // 2)),
-        "b2": lambda: V([R["sl"]], v.transpose, T.b2[:], T.a2[:]),
+        "kb": lambda: A([R["incl"], c_k], T.kb[:], T.kn[:], 1.0, m),
+        "ma": lambda: A([R["incl"]], T.ma[:], m, -1.0, float(HW)),
+        "b2": lambda: V([R["cs"]], v.transpose, T.b2[:], T.a2[:]),
         "xr": lambda: V([R["col0"], R["col1"], R["col2"], R["num"]], v.transpose, T.xr[:], T.xx[:]),
         "dd": lambda: C([R["xr"], vo], T.dd[:], T.xr[:].indirect(T.vo[:])),
-        "et": lambda: V([R["ev%d" % (len(LISTS) - 1)]], v.transpose, T.et[:], T.ee[:, 0:MX]),
+        "gg0": lambda: V(count(0, 8)[1] + [R["ma"]], v.tensor_scalar, T.gg[:], count(0, 8)[0], T.ma[:], float(MX), ALU.is_le, ALU.mult),
+        "uu0": lambda: V([R["gg0"]], v.tensor_tensor, T.uu[:], T.gg[:], count(0, 8)[0], ALU.subtract),
+        "rn0": lambda: V([R["uu0"]], v.tensor_scalar, T.rkn[:], T.uu[:], float(HW), None, ALU.add),
+        "ev0": lambda: V([R["rn0"], z_m, R["dd"]], v.tensor_copy, T.ee[:].indirect(T.rkn[:]), T.dd[:]),
+        "et": lambda: V([R["ev0"]], v.transpose, T.et[:], T.ee[:, 0:MX]),
         "l1": lambda: V([R["et"]], v.tensor_tensor, T.l1[:], T.et[:, :, 0:2], T.et[:, :, 16:18], ALU.add),
         "l2": lambda: V([R["l1"]], v.tensor_tensor, T.l2[0:64, :], T.l1[0:64, :], T.l1[64:128, :], ALU.add),
         "l3": lambda: V([R["l2"], z_3], v.tensor_tensor, T.l3[0:32, 0:16], T.l2[0:32, :], T.l2[32:64, :], ALU.add),
         "l4": lambda: V([R["l3"]], v.transpose, T.l4[0:32, :], T.l3[0:32, :]),
-        "dv": lambda: V([rv[1]], v.tensor_copy, T.dum[:], T.psv[:]),
-        "ds": lambda: S([rs[1]], T.dum[:], T.pss[:], ACT.Copy),
-        "snd": snd, "fl": fl, "ma": ma, "cs": cs, "pb": pb, "num": num,
+        "snd": snd, "fl": fl, "cs": cs, "pb": pb, "num": num,
     }
-    numbered = {"col": col, "msk": msk, "join": join, "eq": eq, "tie": tie, "sum": vsum, "rk": rk, "pt": pt, "tr": tr, "c3": c3,
-                "gg": gg, "uu": uu, "rn": rn, "ev": ev, "pv": pv, "ps": psc, "mm": mm, "y": y, "oc": oc, "ys": ys, "os": os, "eo": eo, "hd": hd, "hs": hs, "hj": hj}
+    numbered = {"col": col, "msk": msk, "join": join, "eq": eq, "tv": tv, "sum": vsum, "hd": hd, "hs": hs, "hj": hj, "rk": rk, "pt": pt,
+                "tr": tr, "c3": c3, "pv": pv, "ps": psc, "mm": mm, "y": y, "oc": oc, "ys": ys, "os": osk, "eo": eo}
     halved = {"dif": dif, "sgn": sgn, "cmp": cmp}
     for name in ORDER.split():
         alt[0] = name.endswith("!")

from concourse.bass import DstId, RemoteDMATransfer
from concourse.mybir import dt, AluOpType as ALU, ActivationFunctionType as ACT

NR, NC, CAP, MX = 4, 1024, 96, 256
LC = CAP // 16
WD = NC + 128
HW = WD // 2
MID = NC + NR * CAP // 2
TINY = 2.0 ** -120
UC = 12
SB = (0, 3, 7)
HALF = {6: 512}
TIES = ((1, 2), (4, 5, 6))
CG = ((0, 3), (1, 2), (4, 5, 6, 7))
PEO = "c0 s0 c1 v0 c2 v1 s1"
LOADS = "y:sn0 s:sn1 y:u y:kc0 y:ks0 y:x y:kc1 y:ks1 y:w"
LISTS = ((0, 6), (6, 8))
PIECES = ((0, 384), (384, 768), (768, 896), (896, 1024))
OCS = ((0,), (1,), (2, 3))
YSS = ((0,), (1,), (2, 3))
ORDER = """
col0! dif3a xq dif0a msk3 col1! pq ps snd cmp1a eq1 msk0 sgn3a eq2 col2! cmp2a hd6 tv0 eq5 fl num cmp5w sgn0a dif7w incl eq4 kb! eq6 cs
msk7 cmp2b cmp4w dif0b dif3b b2 cmp1b pb sgn0b tv1 sum1 sum5 sgn3b sum4 cmp6b hs6 join0 sum2 ma join3 xr sgn7a
rk0 wq pt0 hj6! tr0 sgn7b sum6 c30 join7 pv0 ps0 rk1 ps1 oc0 mm0 pv1 dd gg0 pt1 mm1 oc1 y0 uu0 tr1 rn0 ys0 y1 c31 ev0
ps2 ys1 ps3 pv2 os0! os1 pv3 mm2 et mm3 oc2 y2 y3 os3 l1 l2 os2! ys2 l3 l4 eo1! eo0
"""

SCRATCH = {"psv": ("psum", [128, 1024], "float32"), "pss": ("psum", [128, 1024], "float32"), "py": ("psum", [128, 2048], "float32"),
           "tt": ("sbuf", [128, 32, 32], "float16"), "et": ("sbuf", [128, 8, 32], "float32"), "xx": ("sbuf", [128, 8, 32], "float32"),
           "cm": ("sbuf", [128, 8, 1024], "bfloat16")}
_SPEC = {
    "float8_e4m3fn_x4": "uq 142 urq 128 xq 512 wq 128 sndq 384 winq 1408 aftq 1024",
    "uint8": "us 142 urs 128 xs 512 wsc 128 snds 384 wins 1408 afts 1024",
    "int32": "sn8 24 vo0 8",
    "uint16": "su 24 lf 24 lu 24 ul 8 rkd 16 rkn 8 off 64 vo 8",
    "bfloat16": "ua 568 xt 2048 wt 512 eq 1024 eqs 1024 tri 384 w01 16 fl 384 incl 384 csg 768 "
                + " ".join("sg%d 1152" % i for i in SB) + "".join(" sh%d %d" % x for x in HALF.items()),
    "float16": "scn 4096 pt 256",
    "float32": "acc1 8 acc2 8 a2 64 b2 64 tb 264 ysb 1024 kn 3 kb 3 tj 128 ma 1 js 256 m1 1 xr 256 dd 128 ee 1280 gg 8 uu 8 "
               "l1 16 l2 16 l3 32 l4 32 " + " ".join("df%d 1152" % i for i in SB) + "".join(" dh%d %d" % x for x in HALF.items()),
}
for _d in _SPEC:
    _w = _SPEC[_d].split()
    for _i in range(0, len(_w), 2):
        SCRATCH[_w[_i]] = ("sbuf", [128, int(_w[_i + 1])], _d)
SEMAPHORES = "qv qs qt qg lsn lu0 lk0 lk1 lx lw ltb own sto larr carr sent".split()


def rank_program(g, core, T, topo):
    me = T.rank_of(core)
    if me is None:
        return
    seen, total = {}, {}
    v, queues = g.vector, {"v": g.vector, "s": g.scalar, "t": g.tensor, "g": g, "y": g.sync}
    u8, u32, FL = dt.uint8, dt.uint32, {"allow_small_or_imprecise_dtypes": True}

    def wait(q, deps):
        for name, val in deps:
            if seen.get((q, name), 0) < val:
                queues[q].wait_ge(T.sem[name], val)
                seen[(q, name)] = val

    def tick(name, n):
        total[name] = total.get(name, 0) + n
        return (name, total[name])

    def V(deps, f, *a):
        wait("v", deps); f(*a).then_inc(T.sem.qv, 1); return tick("qv", 1)

    def S(deps, out, in_, func, **k):
        wait("s", deps); g.scalar.activation(out, in_, func, **k).then_inc(T.sem.qs, 1); return tick("qs", 1)

    def P(deps, *a):
        wait("t", deps); g.tensor.matmul_mx(*a).then_inc(T.sem.qt, 1); return tick("qt", 1)

    def G(deps, f, *a, **k):
        wait("g", list(deps) + [("qg", total.get("qg", 0))]); f(*a, **k).then_inc(T.sem.qg, 1); return tick("qg", 1)

    def D(q, deps, sem, out, in_):
        wait(q, deps); queues[q].dma_start(out, in_).then_inc(T.sem[sem], 16); return tick(sem, 16)

    alt = [False]

    def C(deps, out, in_):
        return V(deps, v.tensor_copy, out, in_) if alt[0] else S(deps, out, in_, ACT.Copy)

    def A(deps, out, in_, scale, bias):
        if alt[0]:
            return V(deps, v.tensor_scalar, out, in_, scale, bias, ALU.mult, ALU.add)
        return S(deps, out, in_, ACT.Identity, bias=bias, scale=scale)

    what = {"u": ("lu0", T.ua[:, 4 * UC:4 * UC + 8], T.u[:, 0:8]), "x": ("lx", T.xt[:], T.x[:]), "w": ("lw", T.wt[:], T.w[:])}
    for h in range(2):
        a, b = 512 * h, 512 * h + 512
        what["sn%d" % h] = ("lsn", T.sn8[16 * h:16 * h + 16, :], T.sn[:])
        what["kc%d" % h] = ("lk%d" % h, T.winq[:, a:b].bitcast(u8), T.kc[:, 4 * a:4 * b])
        what["ks%d" % h] = ("lk%d" % h, T.wins[:, a:b], T.ks[:, a:b])
    for x in LOADS.split():
        D(x[0], [], *what[x[2:]])
    sn, u0, xl, wl, kl = ("lsn", 32), ("lu0", 16), ("lx", 16), ("lw", 16), [("lk0", 32), ("lk1", 32)]

    V([], v.memset, T.ua[:, 0:4 * UC], 0.0)
    z_u = V([], v.memset, T.ua[:, 4 * UC + 16:], 0.0)
    z_l = V([], v.memset, T.ul[:], UC)
    V([], v.memset, T.w01[:, 0:1], 0.0)
    z_w = V([], v.memset, T.w01[:, 1:16], 1.0)
    zero = T.ua[:, 64:320]
    c_vo = G([], g.iota, T.vo0[:], [[32, 8]], 0, 1)
    c_j = G([], g.iota, T.tj[:], [[1, 128]], 0, -1, **FL)
    t = V([c_vo], v.tensor_scalar, T.m1[:], T.vo0[:, 0:1], 0.5, -1.0, ALU.is_lt, ALU.mult)
    z_x = S([z_u], T.xx[:], zero, ACT.Copy)
    z_a = S([], T.a2[:], T.ua[:, 64:128], ACT.Copy)
    z_t = S([], T.tb[:], T.ua[:, 64:328], ACT.Identity, bias=-4096.0)
    z_3 = S([], T.l3[0:32, :], T.ua[0:32, 64:96], ACT.Copy)
    z_m = S([t], T.ee[:, 0:MX], zero, ACT.Identity, bias=T.m1[:])
    for a in range(4):
        vo = V([], v.tensor_copy, T.vo[32 * a:32 * a + 32, :], T.vo0[0:32, :])

    for a in range(4):
        lf = V([sn], v.tensor_scalar, T.lf[32 * a:32 * a + 32, :], T.sn8[0:32, :], 1.0, 1.0, ALU.add, ALU.min)
    u1 = V([u0], v.tensor_copy, T.ua[:, 4 * UC + 8:4 * UC + 16], T.ua[:, 4 * UC:4 * UC + 8])
    V([], v.tensor_copy, T.su[0:32, :], T.sn8[0:32, :])
    uq = V([u1, z_u], v.quantize_mx, T.uq[:], T.us[:], T.ua[:])
    V([], v.tensor_copy, T.su[32:64, :], T.sn8[0:32, :])
    ur = V([uq, z_l], v.tensor_copy, T.urq[:].bitcast(u32), T.uq[:].bitcast(u32).indirect(T.ul[:]))
    us = S([uq, z_l], T.urs[:], T.us[:].indirect(T.ul[:]), ACT.Copy)
    others = [d for d in range(NR) if d != me]
    emask = {d: sum(1 << e for e in topo.engines(core, T.cores[d])[2 * i:2 * i + 2]) for i, d in enumerate(others)}

    def send(deps, sem, src, dst):
        wait("g", deps)
        tr = []
        for d in others:
            rid, pid = topo.addr(T.cores[d])[0:2]
            tr.append(RemoteDMATransfer(dst_ids=[DstId(rid=rid, pnc=pid)], dma_engine_mask=emask[d], remote_sem=T.sem[sem],
                                        src=src(d), dst=dst(d)))
        g.remote_dma_fused(tr, local_sem=T.sem.sent)
        tick("sent", 2 * len(others))

    send([lf], "larr", lambda d: T.lf[:, LC * d:LC * d + LC], lambda d: T.lu[:, LC * me:LC * me + LC])
    larr = tick("larr", 2 * len(others))
    fl0 = S([lf, z_w], T.fl[:, CAP * me:CAP * me + CAP], T.w01[:].indirect(T.lf[:, LC * me:LC * me + LC]), ACT.Copy)
    for a in range(2, 4):
        su = V([], v.tensor_copy, T.su[32 * a:32 * a + 32, :], T.sn8[0:32, :])
    t = V([c_j], v.tensor_scalar, T.tri[:, 0:128], T.tj[:], 0.0, None, ALU.is_gt)
    for a in range(1, 3):
        c_t = S([t], T.tri[:, 128 * a:128 * a + 128], T.tri[:, 0:128], ACT.Copy)
    for a in range(4):
        V([], v.tensor_scalar, T.kn[32 * a:32 * a + 32, 0:2], T.vo0[0:32, 0:2], -1.0, -0.5 - 64 * a, ALU.mult, ALU.add)
    c_k = V([], v.memset, T.kn[:, 2:3], -float(HW))
    c_js = G([], g.iota, T.js[:], [[256, 8], [0, 2], [2, 16]], -2 * MID, 2, **FL)

    rv, rs, pc = {}, {}, {}

    def p_cols(k):
        for i, b in enumerate(CG[k]):
            c, o = 128 * b, UC - 4 * i
            pc[k] = P([uq, kl[b // 4]], T.py[:, 512 * k:512 * k + 128], T.winq[:, c:c + 128], T.wins[:, c:c + 128],
                      T.uq[:, o:o + 128], T.us[:, o:o + 128], i == 0, b == CG[k][-1])

    def p_rows(ps, r, h):
        a, b = 512 * h, 512 * h + 512
        r[h] = P([ur, us, kl[h]], ps[:, a:b], T.urq[:], T.urs[:], T.winq[:, a:b], T.wins[:, a:b], True, True)

    for x in PEO.split():
        if x[0] == "c":
            p_cols(int(x[1]))
        else:
            p_rows(*{"v": (T.psv, rv), "s": (T.pss, rs)}[x[0]], int(x[1]))

    R = {}
    w0, own0, m = NC + CAP * me, CAP * me, T.incl[:, NR * CAP - 1:NR * CAP]

    def own_score(i):
        return T.xx[:, i, 1:2]

    def col_of(i):
        return [R["col%d" % k] for k in range(3) if i in CG[k]]

    def tie_of(i):
        return [R["tv%d" % k] for k in range(len(TIES)) if i in TIES[k]]

    def runs(h, cut, first=0):
        a, b = ((0, 512), (512, NC), (0, NC))[h]
        a = max(a, first)
        c = min(max(cut, a), b)
        return [(lo, hi, k) for k, (lo, hi) in enumerate(((a, c), (c, b))) if lo < hi]

    def count(a, b):
        return T.scn[:, 512 * a + 511:512 * b:512], [R["join%d" % i if i in SB else "sum%d" % i] for i in range(a, b)]

    def col(k):
        c = CG[k]
        return C([pc[k], z_x], T.xx[:, c[0]:c[-1] + 1:c[1] - c[0], 1:32:16], T.py[:, 512 * k:512 * k + 4 * len(c):2])

    def dif(i, h):
        for lo, hi, k in runs(h, 128 * i + 128 * (i % 4 == 3)):
            t = S([rs[min(h, 1)]] + col_of(i), T["df%d" % i][:, lo + 128 * k:hi + 128 * k], T.pss[:, lo:hi], ACT.Identity, bias=own_score(i), scale=-1.0)
        return t

    def msk(i):
        df, b, d = T["df%d" % i], 128 * i, [R["dif%d%s" % (i, "ab"[i // 4])]]
        lo, hi = df[:, b:b + 128], df[:, b + 128:b + 256]
        early = lambda src: G(d, g.affine_select, lo, src, [[-1, 128]], ALU.is_gt, -1.0, 0, 1)
        late = lambda src: G(d, g.affine_select, hi, src, [[1, 128]], ALU.is_ge, -1.0, 0, -1)
        if i % 4 == 3:
            late(lo)
            return early(lo)
        early(hi)
        return late(hi)

    def sgn(i, part):
        b, df, sg = 128 * i + 128, T["df%d" % i], T["sg%d" % i]
        if part == 0:
            d = [R["dif%da" % i], R["msk%d" % i]] + ([R["dif%db" % i]] if i > 4 else [])
            return S(d, sg[:, 0:b], df[:, 0:b], ACT.Sign, bias=-TINY, scale=-1.0, accum_out=T.acc1[:, i:i + 1])
        d = [R["dif%da" % i], R["dif%db" % i], R["msk%d" % i]]
        return S(d, sg[:, b:WD], df[:, b:WD], ACT.Sign, bias=TINY, scale=-1.0, accum_out=T.acc2[:, i:i + 1])

    def join(i):
        o = 512 * i + 511
        return V([R["sgn%da" % i], R["sgn%db" % i]], v.tensor_scalar, T.scn[:, o:o + 1], T.acc1[:, i:i + 1], T.acc2[:, i:i + 1], 0.5, ALU.add, ALU.mult)

    def cmp(i, h):
        f = HALF.get(i, 0)
        for lo, hi, k in runs(h, 128 * i + 128, f):
            t = V([rv[min(h, 1)]] + col_of(i), v.tensor_scalar, T.cm[:, i, lo:hi], T.psv[:, lo:hi], own_score(i),
                  (HW - f // 2) / (NC - f) - 1.0, (ALU.is_gt, ALU.is_ge)[k], ALU.add)
        return t

    def eq(i):
        b = 128 * i
        return V([rv[i // 4]] + col_of(i), v.tensor_scalar, T.eq[:, b:b + 128], T.psv[:, b:b + 128], own_score(i), None, ALU.is_equal)

    def tv(i):
        a, b = 128 * TIES[i][0], 128 * TIES[i][-1] + 128
        return V([R["eq%d" % k] for k in TIES[i]] + [c_t], v.tensor_tensor_scan, T.eqs[:, a:b], T.tri[:, 0:b - a], T.eq[:, a:b], 0.0, ALU.mult, ALU.add)

    def hd(i):
        return S([rs[HALF[i] > 512]] + col_of(i), T["dh%d" % i][:], T.pss[:, 0:HALF[i]], ACT.Identity, bias=own_score(i), scale=-1.0)

    def hs(i):
        return S([R["hd%d" % i]], T["sh%d" % i][:], T["dh%d" % i][:], ACT.Sign, bias=-TINY, scale=-1.0, accum_out=T.acc1[:, i:i + 1])

    def hj(i):
        return A([R["hs%d" % i]] + tie_of(i), T.acc2[:, i:i + 1], T.acc1[:, i:i + 1], 0.5, T.eqs[:, 128 * i + 127:128 * i + 128])

    def vsum(i):
        a, o = HALF.get(i, 0), 512 * i + 512
        n = (NC - a) // 2
        d, first = ([R["hj%d" % i]], T.acc2[:, i:i + 1]) if a else ([R["cmp%da" % i]] + tie_of(i), T.eqs[:, 128 * i + 127:128 * i + 128])
        return V(d + [R["cmp%db" % i]], v.tensor_tensor_scan, T.scn[:, o - n:o], T.cm[:, i, a:a + n], T.cm[:, i, a + n:NC], first, ALU.add, ALU.add)

    def snd():
        send([R["pq"]], "carr", lambda d: T.sndq[:, CAP * d:CAP * d + CAP].bitcast(u8), lambda d: T.winq[:, w0:w0 + CAP].bitcast(u8))
        send([R["ps"]], "carr", lambda d: T.snds[:, CAP * d:CAP * d + CAP], lambda d: T.wins[:, w0:w0 + CAP])
        D("y", [R["pq"]], "own", T.winq[:, w0:w0 + CAP].bitcast(u8), T.sndq[:, own0:own0 + CAP].bitcast(u8))
        R["own"] = D("y", [R["ps"]], "own", T.wins[:, w0:w0 + CAP], T.snds[:, own0:own0 + CAP])
        return tick("carr", 4 * len(others))

    def fl():
        t = fl0
        for a, b in ((0, LC * me), (LC * me + LC, LC * NR)):
            if a < b:
                t = C([larr, fl0], T.fl[:, 16 * a:16 * b], T.w01[:].indirect(T.lu[:, a:b]))
        return t

    def cs():
        for h in range(2):
            t = S([R["kb"], z_a], T.csg[:, 384 * h:384 * h + 384], T.incl[:], ACT.Sign, bias=T.kb[:, h:h + 1], scale=-1.0,
                  accum_out=T.a2[:, 32 * h:32 * h + 1])
        return t

    def pb():
        for q in range(8):
            t = D("y", [R["b2"], z_t], "ltb", T.tb[16 * q:16 * q + 1, 1:MX + 1], T.b2[0:128:32, :])
        return t

    def num():
        G([z_x], g.iota, T.xx[:, :, 0:32:16], [[128, 8], [0, 2]], 1, 1, **FL)
        return G([], g.iota, T.xx[0:16, :, 0:32:16], [[128, 8], [0, 2]], 0, 1, **FL)

    def rk(k):
        (a, b), (cnt, d) = LISTS[k], count(*LISTS[k])
        for e in range(2):
            t = V(d + [R["kb"]], v.tensor_scalar, T.rkd[:, 2 * a + e:2 * b:2], cnt, T.kb[:, 2:3], 0.0, ALU.add, ALU.max)
        return t

    def pt(k):
        a, b = LISTS[k]
        return V([R["rk%d" % k], R["pb"], z_t, c_js], v.tensor_tensor, T.pt[:, 32 * a:32 * b], T.tb[:, 0:MX + 1].indirect(T.rkd[:, 2 * a:2 * b]),
                 T.js[:, 32 * a:32 * b], ALU.max)

    def tr(k):
        a, b = LISTS[k]
        for q in range(4):
            t = V([R["pt%d" % k]], v.transpose, T.tt[0:32, 4 * a + q:4 * b:4, :], T.pt[32 * q:32 * q + 32, 32 * a:32 * b])
        return t

    def c3(k):
        a, b = LISTS[k]
        for q in range(4):
            t = V([R["tr%d" % k]], v.tensor_scalar, T.off[32 * q:32 * q + 32, 8 * a:8 * b], T.tt[0:32, 4 * a:4 * b, 0:32:16], 0.5, float(MID),
                  ALU.mult, ALU.add)
        return t

    def have(i):
        return [R["c3%d" % sum(PIECES[i][0] >= 128 * b for a, b in LISTS)], R["own"], R["snd"]] + kl

    def pv(i):
        a, b = PIECES[i]
        return V(have(i), v.tensor_copy, T.aftq[:, a:b].bitcast(u32), T.winq[:].bitcast(u32).indirect(T.off[:, a // 16:b // 16]))

    def psc(i):
        a, b = PIECES[i]
        return C(have(i), T.afts[:, a:b], T.wins[:].indirect(T.off[:, a // 16:b // 16]))

    def mm(i):
        a, b = PIECES[i]
        return P([R["pv%d" % i], R["ps%d" % i], R["wq"], R["col0"], R["col1"], R["col2"]], T.py[:, 512 * i:512 * i + b - a],
                 T.wq[:], T.wsc[:], T.aftq[:, a:b], T.afts[:, a:b], True, True)

    def y(i):
        a, b = PIECES[i]
        return C([R["mm%d" % i]], T.ysb[:, a:b], T.py[:, 512 * i:512 * i + b - a])

    def oc(i):
        a, b = PIECES[OCS[i][0]][0], PIECES[OCS[i][-1]][1]
        return D("ys"[alt[0]], [R["pv%d" % k] for k in OCS[i]], "sto", T.oc[:, 4 * a:4 * b], T.aftq[:, a:b].bitcast(u8))

    def ys(i):
        a, b = PIECES[YSS[i][0]][0], PIECES[YSS[i][-1]][1]
        return D("ys"[alt[0]], [R["y%d" % k] for k in YSS[i]], "sto", T.y[:, a:b], T.ysb[:, a:b])

    def osk(k):
        return D("ys"[alt[0]], [R["ps%d" % i] for i in range(len(PIECES))], "sto", T.osc[4 * k:4 * k + 4, :], T.afts[32 * k:32 * k + 4, :])

    def eo(e):
        return D("ys"[alt[0]], [R["l4"]], "sto", T.ev[e:e + 1, :], T.l4[e:16:2, :])

    plain = {
        "xq": lambda: V([xl], v.quantize_mx, T.xq[:], T.xs[:], T.xt[:]),
        "pq": lambda: V([R["xq"], su], v.tensor_copy, T.sndq[:].bitcast(u32), T.xq[:].bitcast(u32).indirect(T.su[:])),
        "ps": lambda: C([R["xq"], su], T.snds[:], T.xs[:].indirect(T.su[:])),
        "wq": lambda: V([wl], v.quantize_mx, T.wq[:], T.wsc[:], T.wt[:]),
        "incl": lambda: V([R["fl"]], v.tensor_tensor_scan, T.incl[:], T.fl[:], T.fl[:], 0.0, ALU.add, ALU.max),
        "kb": lambda: A([R["incl"], c_k], T.kb[:], T.kn[:], 1.0, m),
        "ma": lambda: A([R["incl"]], T.ma[:], m, -1.0, float(HW)),
        "b2": lambda: V([R["cs"]], v.transpose, T.b2[:], T.a2[:]),
        "xr": lambda: V([R["col0"], R["col1"], R["col2"], R["num"]], v.transpose, T.xr[:], T.xx[:]),
        "dd": lambda: C([R["xr"], vo], T.dd[:], T.xr[:].indirect(T.vo[:])),
        "gg0": lambda: V(count(0, 8)[1] + [R["ma"]], v.tensor_scalar, T.gg[:], count(0, 8)[0], T.ma[:], float(MX), ALU.is_le, ALU.mult),
        "uu0": lambda: V([R["gg0"]], v.tensor_tensor, T.uu[:], T.gg[:], count(0, 8)[0], ALU.subtract),
        "rn0": lambda: V([R["uu0"]], v.tensor_scalar, T.rkn[:], T.uu[:], float(HW), None, ALU.add),
        "ev0": lambda: V([R["rn0"], z_m, R["dd"]], v.tensor_copy, T.ee[:].indirect(T.rkn[:]), T.dd[:]),
        "et": lambda: V([R["ev0"]], v.transpose, T.et[:], T.ee[:, 0:MX]),
        "l1": lambda: V([R["et"]], v.tensor_tensor, T.l1[:], T.et[:, :, 0:2], T.et[:, :, 16:18], ALU.add),
        "l2": lambda: V([R["l1"]], v.tensor_tensor, T.l2[0:64, :], T.l1[0:64, :], T.l1[64:128, :], ALU.add),
        "l3": lambda: V([R["l2"], z_3], v.tensor_tensor, T.l3[0:32, 0:16], T.l2[0:32, :], T.l2[32:64, :], ALU.add),
        "l4": lambda: V([R["l3"]], v.transpose, T.l4[0:32, :], T.l3[0:32, :]),
        "snd": snd, "fl": fl, "cs": cs, "pb": pb, "num": num,
    }
    numbered = {"col": col, "msk": msk, "join": join, "eq": eq, "tv": tv, "sum": vsum, "hd": hd, "hs": hs, "hj": hj, "rk": rk, "pt": pt,
                "tr": tr, "c3": c3, "pv": pv, "ps": psc, "mm": mm, "y": y, "oc": oc, "ys": ys, "os": osk, "eo": eo}
    halved = {"dif": dif, "sgn": sgn, "cmp": cmp}
    for name in ORDER.split():
        alt[0] = name.endswith("!")
        name = name.rstrip("!")
        if name in plain:
            R[name] = plain[name]()
        elif name[-1] in "ab":
            R[name] = halved[name[:-2]](int(name[-2]), "ab".index(name[-1]))
        elif name[-1] == "w":
            R[name[:-1] + "a"] = R[name[:-1] + "b"] = halved[name[:-2]](int(name[-2]), 2)
        else:
            R[name] = numbered[name[:-1]](int(name[-1]))

    for name in SEMAPHORES:
        if name in total:
            wait("g", [(name, total[name])])
